import numpy as np
import ml_dtypes


def mxq(x, axis, fmt="e4m3"):
    dtype, down = {"e4m3": (ml_dtypes.float8_e4m3fn, 7), "e5m2": (ml_dtypes.float8_e5m2, 14)}[fmt]
    v = np.moveaxis(np.asarray(x, np.float32).astype(ml_dtypes.bfloat16).astype(np.float64), axis, -1)
    blocks = v.reshape(v.shape[:-1] + (-1, 32))
    amax = np.abs(blocks).max(-1, keepdims=True)
    byte = np.maximum(np.where(amax > 0, np.frexp(amax)[1] - 1 + 127, 0) - down, 1)
    scale = np.exp2(byte - 127.0)
    codes = (blocks / scale).astype(np.float32).astype(dtype).astype(np.float64)
    return np.moveaxis((codes * scale).reshape(v.shape), -1, axis)


WIDE = False


def mx_kscale(k):
    if not WIDE:
        return np.ones(k)
    levels = np.array([10, -10, 5, -5, 0])
    if k % 512:
        return np.exp2(np.random.permutation(np.resize(levels, k // 32))).repeat(32)
    a = np.empty((k // 512, 16))
    for p in range(k // 512):
        a[p, :8] = np.random.permutation(np.resize(levels, 8))
        for g in range(8):
            far = levels[np.abs(levels - a[p, g]) >= 10]
            a[p, g + 8] = far[np.random.randint(len(far))]
    return np.exp2(a.ravel()).repeat(32)


def f64(x):
    return np.asarray(x).astype(np.float64)


def striped(idx):
    return np.tile(idx.reshape(-1, 16).T, (8, 1)).astype(np.uint16)


def unstriped(offs):
    return offs[:16].T.reshape(-1).astype(np.int64)


E2M1 = np.array([0.0, 0.5, 1.0, 1.5, 2.0, 3.0, 4.0, 6.0, -0.0, -0.5, -1.0, -1.5, -2.0, -3.0, -4.0, -6.0])


def pack_weight(w, fmt):
    k, n = w.shape
    w = f64(np.asarray(w, np.float32).astype(ml_dtypes.bfloat16)).reshape(k // 32, 32, n)
    amax = np.abs(w).max(1)
    if fmt == "e4m3":
        byte = np.frexp(amax)[1] - 1 + 127 - 7
    else:
        mant, ex = np.frexp(amax / 6.0)
        byte = np.where(mant > 0.5, ex, ex - 1) + 127
    byte = np.clip(np.where(amax > 0, byte, 1), 1, 254)
    scaled = (w * np.exp2(127.0 - byte)[:, None, :]).reshape(k, n).astype(np.float32)
    by_word = np.ascontiguousarray(scaled.reshape(k // 512, 128, 4, n).transpose(0, 1, 3, 2))
    if fmt == "e4m3":
        words = by_word.astype(ml_dtypes.float8_e4m3fn).view(np.uint8)
    else:
        c = by_word.astype(ml_dtypes.float4_e2m1fn).view(np.uint8) & 0xF
        words = (c[..., 0::2] | (c[..., 1::2] << 4)).reshape(k // 512, 128, 2 * n)
    return np.ascontiguousarray(words), np.ascontiguousarray(byte.astype(np.uint8).reshape(k // 512, 16, n))


def unpack_weight(words, scales, fmt):
    g, _, n = scales.shape
    words = np.ascontiguousarray(words).reshape(g, 128, n, -1)
    if fmt == "e4m3":
        vals = words.view(ml_dtypes.float8_e4m3fn).astype(np.float64)
    else:
        nib = np.empty((g, 128, n, 4), np.uint8)
        nib[..., 0::2] = words & 0xF
        nib[..., 1::2] = words >> 4
        vals = E2M1[nib]
    vals = vals * np.repeat(np.exp2(scales.astype(np.float64) - 127.0), 8, axis=1)[..., None]
    return vals.transpose(0, 1, 3, 2).reshape(g * 512, n)


def gelu(v):
    return 0.5 * v * (1.0 + np.tanh(np.sqrt(2.0 / np.pi) * (v + 0.044715 * v**3)))


K, T, S, P, H, N = 1024, 4096, 1024, 512, 1024, 768

def setup_inputs():
    n = np.random.standard_normal
    s = mx_kscale(K)[:, None]
    u = mx_kscale(H)[:, None]
    d = {}
    d["tab_words"], d["tab_scales"] = pack_weight(n((K, T)) * s, "e2m1")
    d["offs"] = striped(np.random.permutation(T)[:S])
    d["pos1"] = striped(np.random.permutation(S)[:P])
    d["pos2"] = striped(np.random.permutation(S)[:P])
    d["w1"] = (n((K, H)) / K ** 0.5 / s * u.T).astype(np.float32)
    d["w2_words"], d["w2_scales"] = pack_weight(1.5 * n((K, H)) / K ** 0.5 / s, "e4m3")
    d["gain"] = (np.exp(0.3 * n(H)) * u[:, 0]).astype(np.float32)
    d["steep"] = (2.0 * np.exp(0.2 * n(H)) / u[:, 0]).astype(np.float32)
    d["w3_words"], d["w3_scales"] = pack_weight(n((H, N)) / H ** 0.5 / u, "e2m1")
    return d

def reference(tab_words, tab_scales, offs, pos1, pos2, w1, w2_words, w2_scales, gain, steep, w3_words, w3_scales):
    v = unpack_weight(tab_words, tab_scales, "e2m1")[:, unstriped(offs)]
    w2 = unpack_weight(w2_words, w2_scales, "e4m3")
    w3 = unpack_weight(w3_words, w3_scales, "e2m1")
    lin = mxq(f64(w1), 0, "e4m3").T @ v
    bent = w2.T @ v
    h = lin + f64(gain)[:, None] * (bent / (1.0 + np.exp(-bent)))
    dom = h[:, unstriped(pos1)]
    sup = h[:, unstriped(pos2)]
    arg = f64(steep)[:, None] * sup
    z = dom * (1.0 / (1.0 + np.exp(-arg))) + sup
    return w3.T @ mxq(z, 0, "e4m3")

@@ -1,0 +1,301 @@
+from contextlib import ExitStack
+
+import concourse.mybir as mybir
+from concourse.masks import make_identity
+
+K, T, S, PAIRS, H, N = 1024, 4096, 1024, 512, 1024, 768
+FLOPS = 2 * 2 * K * H * S + 2 * H * N * PAIRS
+
+F32 = mybir.dt.float32
+BF16 = mybir.dt.bfloat16
+I32 = mybir.dt.int32
+U32 = mybir.dt.uint32
+U16 = mybir.dt.uint16
+U8 = mybir.dt.uint8
+FP8X4 = mybir.dt.float8_e4m3fn_x4
+FP4X4 = mybir.dt.float4_e2m1fn_x4
+MULT = mybir.AluOpType.mult
+ADD = mybir.AluOpType.add
+SILU = mybir.ActivationFunctionType.Silu
+SIGMOID = mybir.ActivationFunctionType.Sigmoid
+
+P = 128
+PACK = 4
+K_PASS = P * PACK
+PASSES = 2
+BANK = 512
+R_TILES = H // P
+N_TILES = N // P
+HALVES = S // BANK
+UNIT = 2048
+W1_UNITS = ((10, 11), (1, 2), (4, 5), (10, 11), (6, 7), (8, 9), (1, 2), (4, 5))
+W2_UNITS = (0, 3, 10, 11)
+W3_UNIT = 6
+W2_CHUNK = 2
+GROUPS = (
+    (0, 256, ((0, 1), (2, 3), (4, 5), (6, 7)), (2, 3), ((4, (0, 1)), (5, (2, 3)), (7, (4, 5)))),
+    (256, 128, ((0, 1, 2, 3), (4, 5, 6, 7)), (2, 2), ((6, (0, 1, 2)), (3, (3, 4, 5)))),
+    (384, 128, ((0, 1, 2, 3), (4, 5, 6), (7,)), (2, 2), ((4, (0, 1, 2)), (5, (3, 4, 5)))),
+)
+
+
+def tile_list_handshape_pair_gloss_kernel(
+    tc, tab_words, tab_scales, offs, pos1, pos2, w1, w2_words, w2_scales, gain, steep, w3_words, w3_scales, out
+):
+    nc = tc.nc
+    with ExitStack() as ctx:
+        keep = ctx.enter_context(tc.tile_pool(name="keep", bufs=1))
+        ring = ctx.enter_context(tc.tile_pool(name="ring", bufs=2))
+        arena = ctx.enter_context(tc.tile_pool(name="arena", bufs=1))
+        psum = ctx.enter_context(tc.psum_pool(name="psum", bufs=1))
+        banks = [psum.tile([P, BANK], F32, name=f"bank{b}") for b in range(8)]
+
+        def held(shape, dtype, name):
+            return keep.tile(shape, dtype, name=name, align_bytes=64)
+
+        def placed(shape, dtype, name, unit):
+            return arena.tile(shape, dtype, name=name, align_bytes=64, offset=unit * UNIT)
+
+        offs_sb = keep.tile([P, S // 16], U16, name="offs_sb")
+        pos1_sb = keep.tile([P, PAIRS // 16], U16, name="pos1_sb")
+        pos2_sb = keep.tile([P, PAIRS // 16], U16, name="pos2_sb")
+        tab_scale_rows = placed([P, T], U8, "tab_scale_rows", 0)
+        tab_word_sb = [placed([P, T], U16, f"tab_word{a}", 2 + 4 * a) for a in range(PASSES)]
+        w2_plane = held([P, PASSES, H], U8, "w2_plane")
+        w3_plane = held([P, PASSES, N], U8, "w3_plane")
+        picked_rows = held([P, S], U8, "picked_rows")
+        picked_plane = [held([P, S], U8, f"picked_plane{a}") for a in range(PASSES)]
+        vec_rows = held([P, P], F32, "vec_rows")
+        ident = held([P, P], F32, "ident")
+        gain_col = held([P, R_TILES], F32, "gain_col")
+        steep_col = held([P, R_TILES], F32, "steep_col")
+
+        steep_rows = held([P, P], F32, "steep_rows")
+        zeros = held([P, P], F32, "zeros")
+        nc.vector.memset(zeros[:], 0.0)
+        nc.scalar.activation(vec_rows[:], zeros[:], SILU)
+        nc.scalar.copy(steep_rows[:], zeros[:])
+        nc.vector.memset(w2_plane[:].rearrange("p a c -> p (a c)").bitcast(I32), 0)
+        nc.vector.memset(tab_scale_rows[32:64, :].bitcast(I32), 0)
+        nc.vector.memset(tab_scale_rows[64:P, :].bitcast(I32), 0)
+        for a in range(PASSES):
+            nc.vector.memset(picked_plane[a][:].bitcast(I32), 0)
+        nc.vector.memset(w3_plane[:].rearrange("p a c -> p (a c)").bitcast(I32), 0)
+
+        nc.sync.dma_start(offs_sb[:], offs)
+        nc.sync.dma_start(
+            out=tab_scale_rows[0:32, :].bitcast(I32), in_=tab_scales.rearrange("a q t -> (a q) t").bitcast(I32)
+        )
+        nc.sync.dma_start(pos2_sb[:], pos2)
+        nc.sync.dma_start(pos1_sb[:], pos1)
+        for a in range(PASSES):
+            nc.sync.dma_start(out=tab_word_sb[a][:].bitcast(I32), in_=tab_words[a].bitcast(I32))
+
+        def load_plane(queue, plane, scales):
+            for q in range(4):
+                queue.dma_start(
+                    out=plane[32 * q : 32 * q + 4, :, :].bitcast(I32),
+                    in_=scales[:, 4 * q : 4 * q + 4, :].rearrange("a r c -> r a c").bitcast(I32),
+                )
+
+        load_plane(nc.gpsimd, w2_plane, w2_scales)
+        nc.gpsimd.dma_start(out=vec_rows[0:R_TILES, :], in_=gain.rearrange("(c p) -> c p", p=P))
+        make_identity(nc, ident[:])
+
+        w2_sb = {}
+        w1_raw = {}
+        w2_view = w2_words.rearrange("a p c t -> p a (c t)")
+
+        def load_w2(c0):
+            tile = placed([P, PASSES, W2_CHUNK * P], U32, f"w2_sb{c0}", W2_UNITS[c0 // W2_CHUNK])
+            cols = slice(PACK * P * c0, PACK * P * (c0 + W2_CHUNK))
+            nc.sync.dma_start(out=tile[:].bitcast(I32), in_=w2_view[:, :, cols].bitcast(I32))
+            for i in range(W2_CHUNK):
+                w2_sb[c0 + i] = (tile, i * P)
+
+        def load_w1(c):
+            for a in range(PASSES):
+                tile = placed([P, PACK, P], F32, f"w1_raw{c}_{a}", W1_UNITS[c][a])
+                rows = w1[a * K_PASS : (a + 1) * K_PASS, c * P : (c + 1) * P]
+                nc.sync.dma_start(out=tile[:], in_=rows.rearrange("(p j) c -> p j c", j=PACK))
+                w1_raw[(c, a)] = (tile, 0)
+
+        load_w1(0)
+
+        nc.vector.tensor_copy(picked_rows[:], tab_scale_rows[:].indirect(offs_sb[:]))
+        for a, queue in enumerate((nc.scalar, nc.scalar)):
+            for q in range(4):
+                queue.dma_start(
+                    out=picked_plane[a][32 * q : 32 * q + 4, :].bitcast(I32),
+                    in_=picked_rows[16 * a + 4 * q : 16 * a + 4 * q + 4, :].bitcast(I32),
+                )
+        nc.gpsimd.dma_start(out=steep_rows[0:R_TILES, :], in_=steep.rearrange("(c p) -> c p", p=P))
+        load_plane(nc.gpsimd, w3_plane, w3_scales)
+        load_w2(0)
+        picked = {}
+        for a in range(PASSES):
+            for half in range(HALVES):
+                tile = held([P, BANK], U16, f"picked{a}_{half}")
+                part = offs_sb[:, half * BANK // 16 : (half + 1) * BANK // 16]
+                nc.vector.tensor_copy(tile[:], tab_word_sb[a][:].indirect(part))
+                picked[(a, half)] = tile
+
+        load_w1(1)
+        load_w1(2)
+        load_w2(2)
+
+        w1_bf = {}
+        w1_q = {}
+
+        def round_w1(c):
+            grouped = ring.tile([P, PASSES, P, PACK], BF16, name="w1_grouped", align_bytes=64, bufs=3)
+            for a in range(PASSES):
+                tile, col = w1_raw[(c, a)]
+                nc.scalar.copy(
+                    grouped[:, a, :, :].rearrange("p (c i) j -> p c j i", i=4),
+                    tile[:, :, col : col + P].rearrange("p j (c i) -> p c j i", i=4),
+                )
+            w1_bf[c] = grouped
+
+        def quantize_w1(c):
+            codes = held([P, PASSES * P], U32, f"w1_codes{c}")
+            plane = held([P, PASSES * P], U8, f"w1_plane{c}")
+            nc.vector.quantize_mx(
+                out=codes[:].bitcast(FP8X4), scales=plane[:], in_=w1_bf[c][:].rearrange("p a c j -> p (a c j)")
+            )
+            w1_q[c] = (codes, plane)
+
+        def first_stage(bank, weights, half):
+            cols = slice(half * BANK, (half + 1) * BANK)
+            for a in range(PASSES):
+                codes, plane = weights[a]
+                nc.tensor.matmul_mx(
+                    out=bank[:],
+                    lhsT=codes.bitcast(FP8X4),
+                    lhsT_scale=plane,
+                    rhs=picked[(a, half)][:].bitcast(FP4X4),
+                    rhs_scale=picked_plane[a][:, cols],
+                    start=(a == 0),
+                    stop=(a == PASSES - 1),
+                )
+
+        h = [held([P, S], F32, f"h{c}") for c in range(R_TILES)]
+        sup = [held([P, PAIRS], F32, f"sup{c}") for c in range(R_TILES)]
+        LEAD = 2
+        w3_sb = []
+
+        def load_after(c):
+            if c == 0:
+                load_w1(3)
+                load_w1(4)
+                load_w1(5)
+            if c in (1, 2):
+                load_w1(c + 5)
+            if c == 3:
+                load_w2(4)
+                load_w2(6)
+            if c == 4:
+                tile = placed([P, PASSES, 2 * N], U8, "w3_sb", W3_UNIT)
+                nc.sync.dma_start(out=tile[:].bitcast(I32), in_=w3_words.rearrange("a p b -> p a b").bitcast(I32))
+                w3_sb.append(tile)
+
+        for c in range(LEAD):
+            round_w1(c)
+            load_after(c)
+            quantize_w1(c)
+        for c in range(R_TILES):
+            w2_tile, col = w2_sb[c]
+            w2_ops = [(w2_tile[:, a, col : col + P], w2_plane[:, a, c * P : (c + 1) * P]) for a in range(PASSES)]
+            codes, plane = w1_q[c]
+            w1_ops = [(codes[:, a * P : (a + 1) * P], plane[:, a * P : (a + 1) * P]) for a in range(PASSES)]
+            for half in range(HALVES):
+                bent = banks[4 * (c % 2) + 2 * half]
+                lin = banks[4 * (c % 2) + 2 * half + 1]
+                first_stage(bent, w2_ops, half)
+                first_stage(lin, w1_ops, half)
+                if c == 0 and half == 0:
+                    nc.tensor.transpose(banks[7][:, 0:P], vec_rows[:], ident[:])
+                    nc.scalar.copy(gain_col[:], banks[7][:, 0:R_TILES])
+                act = ring.tile([P, BANK], F32, name="act", bufs=4)
+                nc.scalar.activation(act[:], bent[:], SILU)
+                nc.vector.scalar_tensor_tensor(
+                    h[c][:, half * BANK : (half + 1) * BANK], act[:], gain_col[:, c : c + 1], lin[:], MULT, ADD
+                )
+            if c + LEAD < R_TILES:
+                round_w1(c + LEAD)
+                load_after(c + LEAD)
+                quantize_w1(c + LEAD)
+            nc.vector.tensor_copy(sup[c][:], h[c][:].indirect(pos2_sb[:]))
+
+        nc.tensor.transpose(banks[6][:, 0:P], steep_rows[:], ident[:])
+        nc.scalar.copy(steep_col[:], banks[6][:, 0:R_TILES])
+
+        out_view = out.rearrange("(t p) m -> p t m", p=P)
+        fills = 0
+        for g, (m0, width, chunks, word_banks, out_banks) in enumerate(GROUPS):
+            blocks = width // P
+            z_t = [held([P, blocks, 2, P, 2], BF16, f"z_t{g}_{a}") for a in range(PASSES)]
+            for chunk in chunks:
+                a = chunk[0] // PACK
+                count = len(chunk)
+                bank = banks[fills % 2][:, 0 : blocks * count * P].rearrange("p (b i r) -> p b i r", b=blocks, i=count)
+                fills = fills + 1
+                for i, c in enumerate(chunk):
+                    for b in range(blocks):
+                        cols = slice(m0 + b * P, m0 + (b + 1) * P)
+                        nc.tensor.matmul(
+                            bank[:, b, i, :], sup[c][:, cols], ident[:], start=(i == 0 and b == 0), stop=False,
+                            is_transpose=True,
+                        )
+                for i, c in enumerate(chunk):
+                    gate = held([P, width], F32, f"gate{g}_{c}")
+                    nc.scalar.activation(gate[:], sup[c][:, m0 : m0 + width], SIGMOID, scale=steep_col[:, c : c + 1])
+                    gated = ring.tile([P, width], F32, name="gated", bufs=4)
+                    part = pos1_sb[:, m0 // 16 : (m0 + width) // 16]
+                    nc.vector.tensor_tensor(gated[:], h[c][:].indirect(part), gate[:], MULT)
+                    for b in range(blocks):
+                        nc.tensor.matmul(
+                            bank[:, b, i, :], gated[:, b * P : (b + 1) * P], ident[:], start=False,
+                            stop=(i == count - 1 and b == blocks - 1), is_transpose=True,
+                        )
+                q0 = 32 * (chunk[0] % PACK)
+                nc.scalar.copy(
+                    z_t[a][:, :, :, q0 : q0 + 32 * count, :],
+                    bank.rearrange("p b i (q u e) -> p b u (i q) e", u=2, e=2),
+                )
+                if chunk[-1] % PACK != PACK - 1:
+                    continue
+                words = z_t[a][:].rearrange("p b u q e -> p b u (q e)").bitcast(F32)
+                turned = banks[word_banks[a]][:, 0 : 2 * width].rearrange("p (u m) -> p u m", u=2)
+                for b in range(blocks):
+                    for u in range(2):
+                        nc.tensor.transpose(turned[:, u, b * P : (b + 1) * P], words[:, b, u, :], ident[:])
+                z_bf = held([P, PACK * width], BF16, f"z_bf{g}_{a}")
+                nc.scalar.copy(
+                    z_bf[:].bitcast(F32).rearrange("p (m u) -> p m u", u=2), turned.rearrange("p u m -> p m u")
+                )
+                z_codes = held([P, width], U32, f"z_codes{g}_{a}")
+                z_plane = held([P, width], U8, f"z_plane{g}_{a}")
+                nc.vector.quantize_mx(out=z_codes[:].bitcast(FP8X4), scales=z_plane[:], in_=z_bf[:])
+                for slot, (bank_no, n_tiles) in enumerate(out_banks):
+                    acc = banks[bank_no][:, 0 : len(n_tiles) * width].rearrange("p (t m) -> p t m", m=width)
+                    for i, n in enumerate(n_tiles):
+                        for b in range(blocks):
+                            nc.tensor.matmul_mx(
+                                out=acc[:, i, b * P : (b + 1) * P],
+                                lhsT=w3_sb[0][:, a, 2 * P * n : 2 * P * (n + 1)].bitcast(FP4X4),
+                                lhsT_scale=w3_plane[:, a, P * n : P * (n + 1)],
+                                rhs=z_codes[:, b * P : (b + 1) * P].bitcast(FP8X4),
+                                rhs_scale=z_plane[:, b * P : (b + 1) * P],
+                                start=(a == 0 and i == 0 and b == 0),
+                                stop=(a == PASSES - 1 and i == len(n_tiles) - 1 and b == blocks - 1),
+                            )
+                    if a == PASSES - 1:
+                        result = held([P, len(n_tiles), width], F32, f"result{g}_{slot}")
+                        if g == len(GROUPS) - 1 and slot == 1:
+                            nc.vector.tensor_copy(result[:], acc)
+                        else:
+                            nc.scalar.copy(result[:], acc)
+                        nc.sync.dma_start(
+                            out=out_view[:, n_tiles[0] : n_tiles[-1] + 1, m0 : m0 + width], in_=result[:]
+                        )

@@ -17,7 +17,8 @@ FP4X4 = mybir.dt.float4_e2m1fn_x4
 MULT = mybir.AluOpType.mult
 ADD = mybir.AluOpType.add
 SILU = mybir.ActivationFunctionType.Silu
-SIGMOID = mybir.ActivationFunctionType.Sigmoid
+TANH = mybir.ActivationFunctionType.Tanh
+COPY = mybir.ActivationFunctionType.Copy
 
 P = 128
 PACK = 4
@@ -27,16 +28,20 @@ BANK = 512
 R_TILES = H // P
 N_TILES = N // P
 HALVES = S // BANK
-UNIT = 2048
-W1_UNITS = ((10, 11), (1, 2), (4, 5), (10, 11), (6, 7), (8, 9), (1, 2), (4, 5))
-W2_UNITS = (0, 3, 10, 11)
-W3_UNIT = 6
 W2_CHUNK = 2
-GROUPS = (
-    (0, 256, ((0, 1), (2, 3), (4, 5), (6, 7)), (2, 3), ((4, (0, 1)), (5, (2, 3)), (7, (4, 5)))),
-    (256, 128, ((0, 1, 2, 3), (4, 5, 6, 7)), (2, 2), ((6, (0, 1, 2)), (3, (3, 4, 5)))),
-    (384, 128, ((0, 1, 2, 3), (4, 5, 6), (7,)), (2, 2), ((4, (0, 1, 2)), (5, (3, 4, 5)))),
+PICKS = (
+    (0, 384, tuple((6 + c // 7, (c,)) for c in range(8))),
+    (384, 128, ((1, (0, 1, 2, 3)), (7, (4, 5, 6, 7)))),
 )
+GROUPS = (
+    (0, 256, (7, 6), ((2, (0, 1)), (3, (2, 3)), (4, (4, 5)))),
+    (256, 128, (7, 1), ((5, (0, 1, 2)), (0, (3, 4, 5)))),
+    (384, 128, (6, 1), ((2, (0, 1, 2)), (3, (3, 4, 5)))),
+)
+VEC_BANK = 7
+LEAD = 3
+AFFINE_ON_GPSIMD = True
+ROUND_ON_VECTOR = (1,)
 
 
 def tile_list_handshape_pair_gloss_kernel(
@@ -46,21 +51,17 @@ def tile_list_handshape_pair_gloss_kernel(
     with ExitStack() as ctx:
         keep = ctx.enter_context(tc.tile_pool(name="keep", bufs=1))
         ring = ctx.enter_context(tc.tile_pool(name="ring", bufs=2))
-        arena = ctx.enter_context(tc.tile_pool(name="arena", bufs=1))
         psum = ctx.enter_context(tc.psum_pool(name="psum", bufs=1))
         banks = [psum.tile([P, BANK], F32, name=f"bank{b}") for b in range(8)]
 
         def held(shape, dtype, name):
             return keep.tile(shape, dtype, name=name, align_bytes=64)
 
-        def placed(shape, dtype, name, unit):
-            return arena.tile(shape, dtype, name=name, align_bytes=64, offset=unit * UNIT)
-
         offs_sb = keep.tile([P, S // 16], U16, name="offs_sb")
         pos1_sb = keep.tile([P, PAIRS // 16], U16, name="pos1_sb")
         pos2_sb = keep.tile([P, PAIRS // 16], U16, name="pos2_sb")
-        tab_scale_rows = placed([P, T], U8, "tab_scale_rows", 0)
-        tab_word_sb = [placed([P, T], U16, f"tab_word{a}", 2 + 4 * a) for a in range(PASSES)]
+        tab_scale_rows = held([P, T], U8, "tab_scale_rows")
+        tab_word_sb = [held([P, T], U16, f"tab_word{a}") for a in range(PASSES)]
         w2_plane = held([P, PASSES, H], U8, "w2_plane")
         w3_plane = held([P, PASSES, N], U8, "w3_plane")
         picked_rows = held([P, S], U8, "picked_rows")
@@ -70,24 +71,19 @@ def tile_list_handshape_pair_gloss_kernel(
         gain_col = held([P, R_TILES], F32, "gain_col")
         steep_col = held([P, R_TILES], F32, "steep_col")
 
-        steep_rows = held([P, P], F32, "steep_rows")
         zeros = held([P, P], F32, "zeros")
         nc.vector.memset(zeros[:], 0.0)
         nc.scalar.activation(vec_rows[:], zeros[:], SILU)
-        nc.scalar.copy(steep_rows[:], zeros[:])
         nc.vector.memset(w2_plane[:].rearrange("p a c -> p (a c)").bitcast(I32), 0)
-        nc.vector.memset(tab_scale_rows[32:64, :].bitcast(I32), 0)
-        nc.vector.memset(tab_scale_rows[64:P, :].bitcast(I32), 0)
+        nc.vector.memset(tab_scale_rows[0:96, :].bitcast(I32), 0)
         for a in range(PASSES):
             nc.vector.memset(picked_plane[a][:].bitcast(I32), 0)
         nc.vector.memset(w3_plane[:].rearrange("p a c -> p (a c)").bitcast(I32), 0)
 
         nc.sync.dma_start(offs_sb[:], offs)
         nc.sync.dma_start(
-            out=tab_scale_rows[0:32, :].bitcast(I32), in_=tab_scales.rearrange("a q t -> (a q) t").bitcast(I32)
+            out=tab_scale_rows[96:P, :].bitcast(I32), in_=tab_scales.rearrange("a q t -> (a q) t").bitcast(I32)
         )
-        nc.sync.dma_start(pos2_sb[:], pos2)
-        nc.sync.dma_start(pos1_sb[:], pos1)
         for a in range(PASSES):
             nc.sync.dma_start(out=tab_word_sb[a][:].bitcast(I32), in_=tab_words[a].bitcast(I32))
 
@@ -98,8 +94,9 @@ def tile_list_handshape_pair_gloss_kernel(
                     in_=scales[:, 4 * q : 4 * q + 4, :].rearrange("a r c -> r a c").bitcast(I32),
                 )
 
-        load_plane(nc.gpsimd, w2_plane, w2_scales)
+        load_plane(nc.scalar, w2_plane, w2_scales)
         nc.gpsimd.dma_start(out=vec_rows[0:R_TILES, :], in_=gain.rearrange("(c p) -> c p", p=P))
+        nc.gpsimd.dma_start(out=vec_rows[R_TILES : 2 * R_TILES, :], in_=steep.rearrange("(c p) -> c p", p=P))
         make_identity(nc, ident[:])
 
         w2_sb = {}
@@ -107,7 +104,7 @@ def tile_list_handshape_pair_gloss_kernel(
         w2_view = w2_words.rearrange("a p c t -> p a (c t)")
 
         def load_w2(c0):
-            tile = placed([P, PASSES, W2_CHUNK * P], U32, f"w2_sb{c0}", W2_UNITS[c0 // W2_CHUNK])
+            tile = held([P, PASSES, W2_CHUNK * P], U32, f"w2_sb{c0}")
             cols = slice(PACK * P * c0, PACK * P * (c0 + W2_CHUNK))
             nc.sync.dma_start(out=tile[:].bitcast(I32), in_=w2_view[:, :, cols].bitcast(I32))
             for i in range(W2_CHUNK):
@@ -115,23 +112,22 @@ def tile_list_handshape_pair_gloss_kernel(
 
         def load_w1(c):
             for a in range(PASSES):
-                tile = placed([P, PACK, P], F32, f"w1_raw{c}_{a}", W1_UNITS[c][a])
+                tile = held([P, PACK, P], F32, f"w1_raw{c}_{a}")
                 rows = w1[a * K_PASS : (a + 1) * K_PASS, c * P : (c + 1) * P]
                 nc.sync.dma_start(out=tile[:], in_=rows.rearrange("(p j) c -> p j c", j=PACK))
                 w1_raw[(c, a)] = (tile, 0)
 
+        load_w2(0)
         load_w1(0)
 
         nc.vector.tensor_copy(picked_rows[:], tab_scale_rows[:].indirect(offs_sb[:]))
-        for a, queue in enumerate((nc.scalar, nc.scalar)):
+        for a, queue in ((1, nc.scalar), (0, nc.scalar)):
             for q in range(4):
                 queue.dma_start(
                     out=picked_plane[a][32 * q : 32 * q + 4, :].bitcast(I32),
-                    in_=picked_rows[16 * a + 4 * q : 16 * a + 4 * q + 4, :].bitcast(I32),
+                    in_=picked_rows[96 + 16 * a + 4 * q : 96 + 16 * a + 4 * q + 4, :].bitcast(I32),
                 )
-        nc.gpsimd.dma_start(out=steep_rows[0:R_TILES, :], in_=steep.rearrange("(c p) -> c p", p=P))
         load_plane(nc.gpsimd, w3_plane, w3_scales)
-        load_w2(0)
         picked = {}
         for a in range(PASSES):
             for half in range(HALVES):
@@ -141,17 +137,26 @@ def tile_list_handshape_pair_gloss_kernel(
                 picked[(a, half)] = tile
 
         load_w1(1)
+        nc.sync.dma_start(pos2_sb[:], pos2)
         load_w1(2)
         load_w2(2)
+        nc.sync.dma_start(pos1_sb[:], pos1)
+        for c in range(3, R_TILES):
+            load_w1(c)
+            if c % W2_CHUNK == 0:
+                load_w2(c)
+        w3_sb = held([P, PASSES, 2 * N], U8, "w3_sb")
+        nc.sync.dma_start(out=w3_sb[:].bitcast(I32), in_=w3_words.rearrange("a p b -> p a b").bitcast(I32))
 
         w1_bf = {}
         w1_q = {}
 
         def round_w1(c):
-            grouped = ring.tile([P, PASSES, P, PACK], BF16, name="w1_grouped", align_bytes=64, bufs=3)
+            grouped = ring.tile([P, PASSES, P, PACK], BF16, name="w1_grouped", align_bytes=64, bufs=LEAD + 1)
             for a in range(PASSES):
                 tile, col = w1_raw[(c, a)]
-                nc.scalar.copy(
+                copy = nc.vector.tensor_copy if c in ROUND_ON_VECTOR else nc.scalar.copy
+                copy(
                     grouped[:, a, :, :].rearrange("p (c i) j -> p c j i", i=4),
                     tile[:, :, col : col + P].rearrange("p j (c i) -> p c j i", i=4),
                 )
@@ -181,121 +186,209 @@ def tile_list_handshape_pair_gloss_kernel(
 
         h = [held([P, S], F32, f"h{c}") for c in range(R_TILES)]
         sup = [held([P, PAIRS], F32, f"sup{c}") for c in range(R_TILES)]
-        LEAD = 2
-        w3_sb = []
+        bend = [held([P, PAIRS], F32, f"bend{c}") for c in range(R_TILES)]
+        gate = [held([P, PAIRS], F32, f"gate{c}") for c in range(R_TILES)]
+        acts = held([P, 4, BANK], F32, "acts")
 
-        def load_after(c):
-            if c == 0:
-                load_w1(3)
-                load_w1(4)
-                load_w1(5)
-            if c in (1, 2):
-                load_w1(c + 5)
-            if c == 3:
-                load_w2(4)
-                load_w2(6)
-            if c == 4:
-                tile = placed([P, PASSES, 2 * N], U8, "w3_sb", W3_UNIT)
-                nc.sync.dma_start(out=tile[:].bitcast(I32), in_=w3_words.rearrange("a p b -> p a b").bitcast(I32))
-                w3_sb.append(tile)
-
-        for c in range(LEAD):
+        def prepare_w1(c):
             round_w1(c)
-            load_after(c)
             quantize_w1(c)
-        for c in range(R_TILES):
+
+        def products(c, half):
             w2_tile, col = w2_sb[c]
             w2_ops = [(w2_tile[:, a, col : col + P], w2_plane[:, a, c * P : (c + 1) * P]) for a in range(PASSES)]
             codes, plane = w1_q[c]
             w1_ops = [(codes[:, a * P : (a + 1) * P], plane[:, a * P : (a + 1) * P]) for a in range(PASSES)]
-            for half in range(HALVES):
-                bent = banks[4 * (c % 2) + 2 * half]
-                lin = banks[4 * (c % 2) + 2 * half + 1]
-                first_stage(bent, w2_ops, half)
-                first_stage(lin, w1_ops, half)
-                if c == 0 and half == 0:
-                    nc.tensor.transpose(banks[7][:, 0:P], vec_rows[:], ident[:])
-                    nc.scalar.copy(gain_col[:], banks[7][:, 0:R_TILES])
-                act = ring.tile([P, BANK], F32, name="act", bufs=4)
-                nc.scalar.activation(act[:], bent[:], SILU)
-                nc.vector.scalar_tensor_tensor(
-                    h[c][:, half * BANK : (half + 1) * BANK], act[:], gain_col[:, c : c + 1], lin[:], MULT, ADD
-                )
-            if c + LEAD < R_TILES:
-                round_w1(c + LEAD)
-                load_after(c + LEAD)
-                quantize_w1(c + LEAD)
-            nc.vector.tensor_copy(sup[c][:], h[c][:].indirect(pos2_sb[:]))
+            pair = (HALVES * c + half) % 3
+            first_stage(banks[2 * pair], w2_ops, half)
+            first_stage(banks[2 * pair + 1], w1_ops, half)
 
-        nc.tensor.transpose(banks[6][:, 0:P], steep_rows[:], ident[:])
-        nc.scalar.copy(steep_col[:], banks[6][:, 0:R_TILES])
+        def features(c, half):
+            pair = (HALVES * c + half) % 3
+            act = acts[:, (HALVES * c + half) % 4, :]
+            nc.scalar.activation(act, banks[2 * pair][:], SILU)
+            nc.vector.scalar_tensor_tensor(
+                h[c][:, half * BANK : (half + 1) * BANK], act, gain_col[:, c : c + 1], banks[2 * pair + 1][:],
+                MULT, ADD,
+            )
+
+        def gate_tanh(c, cols):
+            nc.scalar.activation(bend[c][:, cols], sup[c][:, cols], TANH, scale=steep_col[:, c : c + 1])
+
+        def gate_affine(c, cols):
+            if AFFINE_ON_GPSIMD:
+                nc.gpsimd.tensor_scalar(gate[c][:, cols], bend[c][:, cols], 0.5, 0.5, MULT, ADD)
+            else:
+                nc.scalar.activation(gate[c][:, cols], bend[c][:, cols], COPY, bias=0.5, scale=0.5)
 
         out_view = out.rearrange("(t p) m -> p t m", p=P)
-        fills = 0
-        for g, (m0, width, chunks, word_banks, out_banks) in enumerate(GROUPS):
+        z_t = [held([P, PAIRS // P, 2, P, 2], BF16, f"z_t{a}") for a in range(PASSES)]
+        z_q = {}
+        z_bf = {}
+        for g, group in enumerate(GROUPS):
+            for a in range(PASSES):
+                z_bf[(g, a)] = held([P, PACK * group[1]], BF16, f"z_bf{g}_{a}")
+
+        def chunk_of(k, c):
+            width = PICKS[k][1]
+            for bank_no, tiles in PICKS[k][2]:
+                if c in tiles:
+                    cols = width * len(tiles)
+                    view = banks[bank_no][:, 0:cols].rearrange("p (b i r) -> p b i r", b=width // P, i=len(tiles))
+                    return view, tiles
+
+        def gated_place(k, c):
+            m0, width = PICKS[k][0:2]
+            if k == 0 and c + 2 < R_TILES:
+                return acts[:, HALVES * (c % 2), 0:width]
+            if k == 0:
+                return held([P, width], F32, f"gated{c}")[:]
+            if c == 0:
+                return acts[:, 3, 0:width]
+            if c < 3:
+                return gate[R_TILES - 1][:, c * width : (c + 1) * width]
+            return gate[c - 2][:, m0 : m0 + width]
+
+        def weigh(k, c):
+            m0, width = PICKS[k][0:2]
+            bank, tiles = chunk_of(k, c)
+            i = tiles.index(c)
+            for b in range(width // P):
+                cols = slice(m0 + b * P, m0 + (b + 1) * P)
+                nc.tensor.matmul(
+                    bank[:, b, i, :], sup[c][:, cols], ident[:], start=(i == 0 and b == 0), stop=False,
+                    is_transpose=True,
+                )
+            gated = gated_place(k, c)
+            part = pos1_sb[:, m0 // 16 : (m0 + width) // 16]
+            nc.vector.tensor_tensor(gated, h[c][:].indirect(part), gate[c][:, m0 : m0 + width], MULT)
+            for b in range(width // P):
+                nc.tensor.matmul(
+                    bank[:, b, i, :], gated[:, b * P : (b + 1) * P], ident[:], start=False,
+                    stop=(c == tiles[-1] and b == width // P - 1), is_transpose=True,
+                )
+
+        def round_z(k, c):
+            m0, width = PICKS[k][0:2]
+            bank, tiles = chunk_of(k, c)
+            q0 = 32 * (tiles[0] % PACK)
+            nc.scalar.copy(
+                z_t[c // PACK][:, m0 // P : (m0 + width) // P, :, q0 : q0 + 32 * len(tiles), :],
+                bank.rearrange("p b i (q u e) -> p b u (i q) e", u=2, e=2),
+            )
+
+        def turn_back(g, a):
+            m0, width, word_banks = GROUPS[g][0:3]
+            words = z_t[a][:].rearrange("p b u q e -> p b u (q e)").bitcast(F32)
+            turned = banks[word_banks[a]][:, 0 : 2 * width].rearrange("p (u m) -> p u m", u=2)
+            for b in range(width // P):
+                for u in range(2):
+                    nc.tensor.transpose(turned[:, u, b * P : (b + 1) * P], words[:, m0 // P + b, u, :], ident[:])
+            words_out = z_bf[(g, a)][:].bitcast(F32).rearrange("p (m u) -> p m u", u=2)
+            nc.scalar.copy(words_out, turned.rearrange("p u m -> p m u"))
+
+        def quantize_z(g, a):
+            width = GROUPS[g][1]
+            z_codes = held([P, width], U32, f"z_codes{g}_{a}")
+            z_plane = held([P, width], U8, f"z_plane{g}_{a}")
+            nc.vector.quantize_mx(out=z_codes[:].bitcast(FP8X4), scales=z_plane[:], in_=z_bf[(g, a)][:])
+            z_q[(g, a)] = (z_codes, z_plane)
+
+        def second_stage(g, a):
+            m0, width, word_banks, out_banks = GROUPS[g]
             blocks = width // P
-            z_t = [held([P, blocks, 2, P, 2], BF16, f"z_t{g}_{a}") for a in range(PASSES)]
-            for chunk in chunks:
-                a = chunk[0] // PACK
-                count = len(chunk)
-                bank = banks[fills % 2][:, 0 : blocks * count * P].rearrange("p (b i r) -> p b i r", b=blocks, i=count)
-                fills = fills + 1
-                for i, c in enumerate(chunk):
+            z_codes, z_plane = z_q[(g, a)]
+            for slot, (bank_no, n_tiles) in enumerate(out_banks):
+                acc = banks[bank_no][:, 0 : len(n_tiles) * width].rearrange("p (t m) -> p t m", m=width)
+                for i, n in enumerate(n_tiles):
                     for b in range(blocks):
-                        cols = slice(m0 + b * P, m0 + (b + 1) * P)
-                        nc.tensor.matmul(
-                            bank[:, b, i, :], sup[c][:, cols], ident[:], start=(i == 0 and b == 0), stop=False,
-                            is_transpose=True,
+                        nc.tensor.matmul_mx(
+                            out=acc[:, i, b * P : (b + 1) * P],
+                            lhsT=w3_sb[:, a, 2 * P * n : 2 * P * (n + 1)].bitcast(FP4X4),
+                            lhsT_scale=w3_plane[:, a, P * n : P * (n + 1)],
+                            rhs=z_codes[:, b * P : (b + 1) * P].bitcast(FP8X4),
+                            rhs_scale=z_plane[:, b * P : (b + 1) * P],
+                            start=(a == 0 and i == 0 and b == 0),
+                            stop=(a == PASSES - 1 and i == len(n_tiles) - 1 and b == blocks - 1),
                         )
-                for i, c in enumerate(chunk):
-                    gate = held([P, width], F32, f"gate{g}_{c}")
-                    nc.scalar.activation(gate[:], sup[c][:, m0 : m0 + width], SIGMOID, scale=steep_col[:, c : c + 1])
-                    gated = ring.tile([P, width], F32, name="gated", bufs=4)
-                    part = pos1_sb[:, m0 // 16 : (m0 + width) // 16]
-                    nc.vector.tensor_tensor(gated[:], h[c][:].indirect(part), gate[:], MULT)
-                    for b in range(blocks):
-                        nc.tensor.matmul(
-                            bank[:, b, i, :], gated[:, b * P : (b + 1) * P], ident[:], start=False,
-                            stop=(i == count - 1 and b == blocks - 1), is_transpose=True,
-                        )
-                q0 = 32 * (chunk[0] % PACK)
-                nc.scalar.copy(
-                    z_t[a][:, :, :, q0 : q0 + 32 * count, :],
-                    bank.rearrange("p b i (q u e) -> p b u (i q) e", u=2, e=2),
-                )
-                if chunk[-1] % PACK != PACK - 1:
-                    continue
-                words = z_t[a][:].rearrange("p b u q e -> p b u (q e)").bitcast(F32)
-                turned = banks[word_banks[a]][:, 0 : 2 * width].rearrange("p (u m) -> p u m", u=2)
-                for b in range(blocks):
-                    for u in range(2):
-                        nc.tensor.transpose(turned[:, u, b * P : (b + 1) * P], words[:, b, u, :], ident[:])
-                z_bf = held([P, PACK * width], BF16, f"z_bf{g}_{a}")
-                nc.scalar.copy(
-                    z_bf[:].bitcast(F32).rearrange("p (m u) -> p m u", u=2), turned.rearrange("p u m -> p m u")
-                )
-                z_codes = held([P, width], U32, f"z_codes{g}_{a}")
-                z_plane = held([P, width], U8, f"z_plane{g}_{a}")
-                nc.vector.quantize_mx(out=z_codes[:].bitcast(FP8X4), scales=z_plane[:], in_=z_bf[:])
-                for slot, (bank_no, n_tiles) in enumerate(out_banks):
-                    acc = banks[bank_no][:, 0 : len(n_tiles) * width].rearrange("p (t m) -> p t m", m=width)
-                    for i, n in enumerate(n_tiles):
-                        for b in range(blocks):
-                            nc.tensor.matmul_mx(
-                                out=acc[:, i, b * P : (b + 1) * P],
-                                lhsT=w3_sb[0][:, a, 2 * P * n : 2 * P * (n + 1)].bitcast(FP4X4),
-                                lhsT_scale=w3_plane[:, a, P * n : P * (n + 1)],
-                                rhs=z_codes[:, b * P : (b + 1) * P].bitcast(FP8X4),
-                                rhs_scale=z_plane[:, b * P : (b + 1) * P],
-                                start=(a == 0 and i == 0 and b == 0),
-                                stop=(a == PASSES - 1 and i == len(n_tiles) - 1 and b == blocks - 1),
-                            )
-                    if a == PASSES - 1:
-                        result = held([P, len(n_tiles), width], F32, f"result{g}_{slot}")
-                        if g == len(GROUPS) - 1 and slot == 1:
-                            nc.vector.tensor_copy(result[:], acc)
-                        else:
-                            nc.scalar.copy(result[:], acc)
-                        nc.sync.dma_start(
-                            out=out_view[:, n_tiles[0] : n_tiles[-1] + 1, m0 : m0 + width], in_=result[:]
-                        )
+
+        def store(g, slots):
+            m0, width, word_banks, out_banks = GROUPS[g]
+            for slot in slots:
+                bank_no, n_tiles = out_banks[slot]
+                acc = banks[bank_no][:, 0 : len(n_tiles) * width].rearrange("p (t m) -> p t m", m=width)
+                result = held([P, len(n_tiles), width], F32, f"result{g}_{slot}")
+                if (g, slot) in ((0, 1), (1, 0), (2, 1)):
+                    nc.vector.tensor_copy(result[:], acc)
+                else:
+                    nc.scalar.copy(result[:], acc)
+                nc.sync.dma_start(out=out_view[:, n_tiles[0] : n_tiles[-1] + 1, m0 : m0 + width], in_=result[:])
+
+        every = slice(0, PAIRS)
+
+        prepare_w1(0)
+        prepare_w1(1)
+        products(0, 0)
+        nc.tensor.transpose(banks[VEC_BANK][:, 0:P], vec_rows[:], ident[:])
+        nc.scalar.copy(gain_col[:], banks[VEC_BANK][:, 0:R_TILES])
+        nc.scalar.activation(steep_col[:], banks[VEC_BANK][:, R_TILES : 2 * R_TILES], COPY, scale=0.5)
+        products(0, 1)
+        for c in range(2, LEAD):
+            prepare_w1(c)
+        for c in range(R_TILES):
+            casting = c + LEAD < R_TILES
+            features(c, 0)
+            if c + 1 < R_TILES:
+                products(c + 1, 0)
+            features(c, 1)
+            if c >= 1:
+                gate_tanh(c - 1, every)
+                gate_affine(c - 1, every)
+            if 3 <= c <= R_TILES - LEAD:
+                round_z(0, c - 3)
+            if c == PACK + 2:
+                turn_back(0, 0)
+                turn_back(1, 0)
+            if c >= 2:
+                weigh(0, c - 2)
+            if c == PACK + 3:
+                quantize_z(1, 0)
+            nc.vector.tensor_copy(sup[c][:], h[c][:].indirect(pos2_sb[:]))
+            if c + 1 < R_TILES:
+                products(c + 1, 1)
+            if casting:
+                prepare_w1(c + LEAD)
+            else:
+                round_z(0, c - 2)
+            if c == PACK + 2:
+                quantize_z(0, 0)
+        second_stage(0, 0)
+        second_stage(1, 0)
+        gate_tanh(7, every)
+        gate_affine(7, every)
+        weigh(0, 6)
+        round_z(0, 6)
+        weigh(1, 0)
+        weigh(0, 7)
+        round_z(0, 7)
+        for c in range(1, PACK):
+            weigh(1, c)
+        turn_back(0, 1)
+        round_z(1, 3)
+        for c in range(PACK, R_TILES):
+            weigh(1, c)
+        turn_back(1, 1)
+        quantize_z(0, 1)
+        round_z(1, 7)
+        turn_back(2, 0)
+        turn_back(2, 1)
+        second_stage(0, 1)
+        quantize_z(1, 1)
+        second_stage(1, 1)
+        quantize_z(2, 0)
+        quantize_z(2, 1)
+        store(0, (0, 1, 2))
+        second_stage(2, 0)
+        second_stage(2, 1)
+        store(1, (0, 1))
+        store(2, (0, 1))

@@ -39,9 +39,9 @@ GROUPS = (
     (384, 128, (6, 1), ((2, (0, 1, 2)), (3, (3, 4, 5)))),
 )
 VEC_BANK = 7
-LEAD = 3
-AFFINE_ON_GPSIMD = True
-ROUND_ON_VECTOR = (1,)
+LEAD = 2
+AFFINE_ON_GPSIMD = False
+ROUND_ON_VECTOR = ()
 
 
 def tile_list_handshape_pair_gloss_kernel(
@@ -95,8 +95,8 @@ def tile_list_handshape_pair_gloss_kernel(
                 )
 
         load_plane(nc.scalar, w2_plane, w2_scales)
-        nc.gpsimd.dma_start(out=vec_rows[0:R_TILES, :], in_=gain.rearrange("(c p) -> c p", p=P))
-        nc.gpsimd.dma_start(out=vec_rows[R_TILES : 2 * R_TILES, :], in_=steep.rearrange("(c p) -> c p", p=P))
+        nc.scalar.dma_start(out=vec_rows[0:R_TILES, :], in_=gain.rearrange("(c p) -> c p", p=P))
+        nc.scalar.dma_start(out=vec_rows[R_TILES : 2 * R_TILES, :], in_=steep.rearrange("(c p) -> c p", p=P))
         make_identity(nc, ident[:])
 
         w2_sb = {}
@@ -127,7 +127,6 @@ def tile_list_handshape_pair_gloss_kernel(
                     out=picked_plane[a][32 * q : 32 * q + 4, :].bitcast(I32),
                     in_=picked_rows[96 + 16 * a + 4 * q : 96 + 16 * a + 4 * q + 4, :].bitcast(I32),
                 )
-        load_plane(nc.gpsimd, w3_plane, w3_scales)
         picked = {}
         for a in range(PASSES):
             for half in range(HALVES):
@@ -147,6 +146,7 @@ def tile_list_handshape_pair_gloss_kernel(
                 load_w2(c)
         w3_sb = held([P, PASSES, 2 * N], U8, "w3_sb")
         nc.sync.dma_start(out=w3_sb[:].bitcast(I32), in_=w3_words.rearrange("a p b -> p a b").bitcast(I32))
+        load_plane(nc.sync, w3_plane, w3_scales)
 
         w1_bf = {}
         w1_q = {}
@@ -194,14 +194,14 @@ def tile_list_handshape_pair_gloss_kernel(
             round_w1(c)
             quantize_w1(c)
 
-        def products(c, half):
+        def products(c, half, parts=(0, 1)):
             w2_tile, col = w2_sb[c]
             w2_ops = [(w2_tile[:, a, col : col + P], w2_plane[:, a, c * P : (c + 1) * P]) for a in range(PASSES)]
             codes, plane = w1_q[c]
             w1_ops = [(codes[:, a * P : (a + 1) * P], plane[:, a * P : (a + 1) * P]) for a in range(PASSES)]
             pair = (HALVES * c + half) % 3
-            first_stage(banks[2 * pair], w2_ops, half)
-            first_stage(banks[2 * pair + 1], w1_ops, half)
+            for part in parts:
+                first_stage(banks[2 * pair + part], (w2_ops, w1_ops)[part], half)
 
         def features(c, half):
             pair = (HALVES * c + half) % 3
@@ -328,11 +328,12 @@ def tile_list_handshape_pair_gloss_kernel(
 
         prepare_w1(0)
         prepare_w1(1)
-        products(0, 0)
         nc.tensor.transpose(banks[VEC_BANK][:, 0:P], vec_rows[:], ident[:])
         nc.scalar.copy(gain_col[:], banks[VEC_BANK][:, 0:R_TILES])
         nc.scalar.activation(steep_col[:], banks[VEC_BANK][:, R_TILES : 2 * R_TILES], COPY, scale=0.5)
-        products(0, 1)
+        for part in range(2):
+            for half in range(HALVES):
+                products(0, half, (part,))
         for c in range(2, LEAD):
             prepare_w1(c)
         for c in range(R_TILES):

@@ -29,19 +29,15 @@ R_TILES = H // P
 N_TILES = N // P
 HALVES = S // BANK
 W2_CHUNK = 2
-PICKS = (
-    (0, 384, tuple((6 + c // 7, (c,)) for c in range(8))),
-    (384, 128, ((1, (0, 1, 2, 3)), (7, (4, 5, 6, 7)))),
-)
-GROUPS = (
-    (0, 256, (7, 6), ((2, (0, 1)), (3, (2, 3)), (4, (4, 5)))),
-    (256, 128, (7, 1), ((5, (0, 1, 2)), (0, (3, 4, 5)))),
-    (384, 128, (6, 1), ((2, (0, 1, 2)), (3, (3, 4, 5)))),
-)
-VEC_BANK = 7
 LEAD = 2
-AFFINE_ON_GPSIMD = False
-ROUND_ON_VECTOR = ()
+ON_VECTOR = ((1, 0), (1, 1))
+BLOCKS = PAIRS // P
+EARLY = 2 * P
+LAST = R_TILES - 1
+SUM_BANKS = (6, 7)
+VEC_BANK = 7
+EARLY_OUT = (2, 3, 4)
+LATE = ((2, 1, 1, (5, 0)), (3, 6, 7, (1, 7)))
 
 
 def tile_list_handshape_pair_gloss_kernel(
@@ -121,7 +117,7 @@ def tile_list_handshape_pair_gloss_kernel(
         load_w1(0)
 
         nc.vector.tensor_copy(picked_rows[:], tab_scale_rows[:].indirect(offs_sb[:]))
-        for a, queue in ((1, nc.scalar), (0, nc.scalar)):
+        for a, queue in ((0, nc.scalar), (1, nc.scalar)):
             for q in range(4):
                 queue.dma_start(
                     out=picked_plane[a][32 * q : 32 * q + 4, :].bitcast(I32),
@@ -155,7 +151,7 @@ def tile_list_handshape_pair_gloss_kernel(
             grouped = ring.tile([P, PASSES, P, PACK], BF16, name="w1_grouped", align_bytes=64, bufs=LEAD + 1)
             for a in range(PASSES):
                 tile, col = w1_raw[(c, a)]
-                copy = nc.vector.tensor_copy if c in ROUND_ON_VECTOR else nc.scalar.copy
+                copy = nc.vector.tensor_copy if (c, a) in ON_VECTOR else nc.scalar.copy
                 copy(
                     grouped[:, a, :, :].rearrange("p (c i) j -> p c j i", i=4),
                     tile[:, :, col : col + P].rearrange("p j (c i) -> p c j i", i=4),
@@ -170,9 +166,9 @@ def tile_list_handshape_pair_gloss_kernel(
             )
             w1_q[c] = (codes, plane)
 
-        def first_stage(bank, weights, half):
+        def first_stage(bank, weights, half, order):
             cols = slice(half * BANK, (half + 1) * BANK)
-            for a in range(PASSES):
+            for a in order:
                 codes, plane = weights[a]
                 nc.tensor.matmul_mx(
                     out=bank[:],
@@ -180,8 +176,8 @@ def tile_list_handshape_pair_gloss_kernel(
                     lhsT_scale=plane,
                     rhs=picked[(a, half)][:].bitcast(FP4X4),
                     rhs_scale=picked_plane[a][:, cols],
-                    start=(a == 0),
-                    stop=(a == PASSES - 1),
+                    start=(a == order[0]),
+                    stop=(a == order[-1]),
                 )
 
         h = [held([P, S], F32, f"h{c}") for c in range(R_TILES)]
@@ -201,7 +197,7 @@ def tile_list_handshape_pair_gloss_kernel(
             w1_ops = [(codes[:, a * P : (a + 1) * P], plane[:, a * P : (a + 1) * P]) for a in range(PASSES)]
             pair = (HALVES * c + half) % 3
             for part in parts:
-                first_stage(banks[2 * pair + part], (w2_ops, w1_ops)[part], half)
+                first_stage(banks[2 * pair + part], (w2_ops, w1_ops)[part], half, ((0, 1), (1, 0))[part])
 
         def features(c, half):
             pair = (HALVES * c + half) % 3
@@ -212,119 +208,118 @@ def tile_list_handshape_pair_gloss_kernel(
                 MULT, ADD,
             )
 
-        def gate_tanh(c, cols):
+        def make_gate(c, cols):
             nc.scalar.activation(bend[c][:, cols], sup[c][:, cols], TANH, scale=steep_col[:, c : c + 1])
+            nc.scalar.activation(gate[c][:, cols], bend[c][:, cols], COPY, bias=0.5, scale=0.5)
 
-        def gate_affine(c, cols):
-            if AFFINE_ON_GPSIMD:
-                nc.gpsimd.tensor_scalar(gate[c][:, cols], bend[c][:, cols], 0.5, 0.5, MULT, ADD)
-            else:
-                nc.scalar.activation(gate[c][:, cols], bend[c][:, cols], COPY, bias=0.5, scale=0.5)
+        def pick_sup(c, cols):
+            part = pos2_sb[:, cols.start // 16 : cols.stop // 16]
+            nc.vector.tensor_copy(sup[c][:, cols], h[c][:].indirect(part))
 
         out_view = out.rearrange("(t p) m -> p t m", p=P)
-        z_t = [held([P, PAIRS // P, 2, P, 2], BF16, f"z_t{a}") for a in range(PASSES)]
+        z_t = [held([P, BLOCKS, 2, P, 2], BF16, f"z_t{a}") for a in range(PASSES)]
         z_q = {}
-        z_bf = {}
-        for g, group in enumerate(GROUPS):
-            for a in range(PASSES):
-                z_bf[(g, a)] = held([P, PACK * group[1]], BF16, f"z_bf{g}_{a}")
 
-        def chunk_of(k, c):
-            width = PICKS[k][1]
-            for bank_no, tiles in PICKS[k][2]:
-                if c in tiles:
-                    cols = width * len(tiles)
-                    view = banks[bank_no][:, 0:cols].rearrange("p (b i r) -> p b i r", b=width // P, i=len(tiles))
-                    return view, tiles
+        def sum_view(bank_no, tiles, cols):
+            blocks = (cols.stop - cols.start) // P
+            used = banks[bank_no][:, 0 : blocks * len(tiles) * P]
+            return used.rearrange("p (b i r) -> p b i r", b=blocks, i=len(tiles))
 
-        def gated_place(k, c):
-            m0, width = PICKS[k][0:2]
-            if k == 0 and c + 2 < R_TILES:
-                return acts[:, HALVES * (c % 2), 0:width]
-            if k == 0:
-                return held([P, width], F32, f"gated{c}")[:]
-            if c == 0:
-                return acts[:, 3, 0:width]
-            if c < 3:
-                return gate[R_TILES - 1][:, c * width : (c + 1) * width]
-            return gate[c - 2][:, m0 : m0 + width]
+        def open_sum(bank_no, tiles, cols):
+            view = sum_view(bank_no, tiles, cols)
+            for i, c in enumerate(tiles):
+                for b, m in enumerate(range(cols.start, cols.stop, P)):
+                    nc.tensor.matmul(
+                        view[:, b, i, :], sup[c][:, m : m + P], ident[:], start=(i == 0 and b == 0), stop=False,
+                        is_transpose=True,
+                    )
 
-        def weigh(k, c):
-            m0, width = PICKS[k][0:2]
-            bank, tiles = chunk_of(k, c)
-            i = tiles.index(c)
-            for b in range(width // P):
-                cols = slice(m0 + b * P, m0 + (b + 1) * P)
+        def weigh(c, gated, bank_no, tiles, cols):
+            view = sum_view(bank_no, tiles, cols)
+            blocks = (cols.stop - cols.start) // P
+            part = pos1_sb[:, cols.start // 16 : cols.stop // 16]
+            nc.vector.tensor_tensor(gated, h[c][:].indirect(part), gate[c][:, cols], MULT)
+            for b in range(blocks):
                 nc.tensor.matmul(
-                    bank[:, b, i, :], sup[c][:, cols], ident[:], start=(i == 0 and b == 0), stop=False,
-                    is_transpose=True,
-                )
-            gated = gated_place(k, c)
-            part = pos1_sb[:, m0 // 16 : (m0 + width) // 16]
-            nc.vector.tensor_tensor(gated, h[c][:].indirect(part), gate[c][:, m0 : m0 + width], MULT)
-            for b in range(width // P):
-                nc.tensor.matmul(
-                    bank[:, b, i, :], gated[:, b * P : (b + 1) * P], ident[:], start=False,
-                    stop=(c == tiles[-1] and b == width // P - 1), is_transpose=True,
+                    view[:, b, tiles.index(c), :], gated[:, b * P : (b + 1) * P], ident[:], start=False,
+                    stop=(c == tiles[-1] and b == blocks - 1), is_transpose=True,
                 )
 
-        def round_z(k, c):
-            m0, width = PICKS[k][0:2]
-            bank, tiles = chunk_of(k, c)
+        def round_z(bank_no, tiles, cols):
             q0 = 32 * (tiles[0] % PACK)
             nc.scalar.copy(
-                z_t[c // PACK][:, m0 // P : (m0 + width) // P, :, q0 : q0 + 32 * len(tiles), :],
-                bank.rearrange("p b i (q u e) -> p b u (i q) e", u=2, e=2),
+                z_t[tiles[0] // PACK][:, cols.start // P : cols.stop // P, :, q0 : q0 + 32 * len(tiles), :],
+                sum_view(bank_no, tiles, cols).rearrange("p b i (q u e) -> p b u (i q) e", u=2, e=2),
             )
 
-        def turn_back(g, a):
-            m0, width, word_banks = GROUPS[g][0:3]
+        z_bf = {}
+
+        def turn_back(a, bank_no, cols):
+            width = cols.stop - cols.start
             words = z_t[a][:].rearrange("p b u q e -> p b u (q e)").bitcast(F32)
-            turned = banks[word_banks[a]][:, 0 : 2 * width].rearrange("p (u m) -> p u m", u=2)
+            turned = banks[bank_no][:, 0 : 2 * width].rearrange("p (u m) -> p u m", u=2)
             for b in range(width // P):
                 for u in range(2):
-                    nc.tensor.transpose(turned[:, u, b * P : (b + 1) * P], words[:, m0 // P + b, u, :], ident[:])
-            words_out = z_bf[(g, a)][:].bitcast(F32).rearrange("p (m u) -> p m u", u=2)
-            nc.scalar.copy(words_out, turned.rearrange("p u m -> p m u"))
+                    nc.tensor.transpose(
+                        turned[:, u, b * P : (b + 1) * P], words[:, cols.start // P + b, u, :], ident[:]
+                    )
+            tile = held([P, PACK * width], BF16, f"z_bf{a}_{cols.start}")
+            nc.scalar.copy(
+                tile[:].bitcast(F32).rearrange("p (m u) -> p m u", u=2), turned.rearrange("p u m -> p m u")
+            )
+            z_bf[(a, cols.start)] = tile
 
-        def quantize_z(g, a):
-            width = GROUPS[g][1]
-            z_codes = held([P, width], U32, f"z_codes{g}_{a}")
-            z_plane = held([P, width], U8, f"z_plane{g}_{a}")
-            nc.vector.quantize_mx(out=z_codes[:].bitcast(FP8X4), scales=z_plane[:], in_=z_bf[(g, a)][:])
-            z_q[(g, a)] = (z_codes, z_plane)
+        def quantize_z(a, cols):
+            width = cols.stop - cols.start
+            z_codes = held([P, width], U32, f"z_codes{a}_{cols.start}")
+            z_plane = held([P, width], U8, f"z_plane{a}_{cols.start}")
+            nc.vector.quantize_mx(out=z_codes[:].bitcast(FP8X4), scales=z_plane[:], in_=z_bf[(a, cols.start)][:])
+            for b in range(width // P):
+                z_q[(a, cols.start // P + b)] = (z_codes[:, b * P : (b + 1) * P], z_plane[:, b * P : (b + 1) * P])
 
-        def second_stage(g, a):
-            m0, width, word_banks, out_banks = GROUPS[g]
-            blocks = width // P
-            z_codes, z_plane = z_q[(g, a)]
-            for slot, (bank_no, n_tiles) in enumerate(out_banks):
-                acc = banks[bank_no][:, 0 : len(n_tiles) * width].rearrange("p (t m) -> p t m", m=width)
-                for i, n in enumerate(n_tiles):
+        def result_view(bank_no, out_banks, cols):
+            width = cols.stop - cols.start
+            per_bank = N_TILES // len(out_banks)
+            return banks[bank_no][:, 0 : per_bank * width].rearrange("p (t m) -> p t m", m=width)
+
+        def second_stage(a, out_banks, cols):
+            blocks = (cols.stop - cols.start) // P
+            per_bank = N_TILES // len(out_banks)
+            for slot, bank_no in enumerate(out_banks):
+                acc = result_view(bank_no, out_banks, cols)
+                for i in range(per_bank):
+                    n = slot * per_bank + i
                     for b in range(blocks):
+                        z_codes, z_plane = z_q[(a, cols.start // P + b)]
                         nc.tensor.matmul_mx(
                             out=acc[:, i, b * P : (b + 1) * P],
                             lhsT=w3_sb[:, a, 2 * P * n : 2 * P * (n + 1)].bitcast(FP4X4),
                             lhsT_scale=w3_plane[:, a, P * n : P * (n + 1)],
-                            rhs=z_codes[:, b * P : (b + 1) * P].bitcast(FP8X4),
-                            rhs_scale=z_plane[:, b * P : (b + 1) * P],
+                            rhs=z_codes.bitcast(FP8X4),
+                            rhs_scale=z_plane,
                             start=(a == 0 and i == 0 and b == 0),
-                            stop=(a == PASSES - 1 and i == len(n_tiles) - 1 and b == blocks - 1),
+                            stop=(a == PASSES - 1 and i == per_bank - 1 and b == blocks - 1),
                         )
 
-        def store(g, slots):
-            m0, width, word_banks, out_banks = GROUPS[g]
-            for slot in slots:
-                bank_no, n_tiles = out_banks[slot]
-                acc = banks[bank_no][:, 0 : len(n_tiles) * width].rearrange("p (t m) -> p t m", m=width)
-                result = held([P, len(n_tiles), width], F32, f"result{g}_{slot}")
-                if (g, slot) in ((0, 1), (1, 0), (2, 1)):
-                    nc.vector.tensor_copy(result[:], acc)
-                else:
-                    nc.scalar.copy(result[:], acc)
-                nc.sync.dma_start(out=out_view[:, n_tiles[0] : n_tiles[-1] + 1, m0 : m0 + width], in_=result[:])
+        def store(out_banks, cols, copies):
+            per_bank = N_TILES // len(out_banks)
+            for slot, bank_no in enumerate(out_banks):
+                result = held([P, per_bank, cols.stop - cols.start], F32, f"result{cols.start}_{slot}")
+                copies[slot](result[:], result_view(bank_no, out_banks, cols))
+                nc.sync.dma_start(out=out_view[:, slot * per_bank : (slot + 1) * per_bank, cols], in_=result[:])
 
-        every = slice(0, PAIRS)
+        every, early, late = slice(0, PAIRS), slice(0, EARLY), slice(EARLY, PAIRS)
+
+        def loop_cols(c):
+            return every if c < PACK else early
+
+        def loop_weigh(c, slot):
+            cols = loop_cols(c)
+            open_sum(SUM_BANKS[c % 2], (c,), cols)
+            weigh(c, acts[:, slot, 0 : cols.stop], SUM_BANKS[c % 2], (c,), cols)
+
+        def loop_round(c):
+            round_z(SUM_BANKS[c % 2], (c,), loop_cols(c))
 
         prepare_w1(0)
         prepare_w1(1)
@@ -334,62 +329,64 @@ def tile_list_handshape_pair_gloss_kernel(
         for part in range(2):
             for half in range(HALVES):
                 products(0, half, (part,))
-        for c in range(2, LEAD):
-            prepare_w1(c)
         for c in range(R_TILES):
-            casting = c + LEAD < R_TILES
             features(c, 0)
-            if c + 1 < R_TILES:
+            if c < LAST:
                 products(c + 1, 0)
             features(c, 1)
             if c >= 1:
-                gate_tanh(c - 1, every)
-                gate_affine(c - 1, every)
-            if 3 <= c <= R_TILES - LEAD:
-                round_z(0, c - 3)
+                make_gate(c - 1, every)
+            if c >= 3:
+                loop_round(c - 3)
             if c == PACK + 2:
-                turn_back(0, 0)
-                turn_back(1, 0)
+                turn_back(0, SUM_BANKS[0], early)
+                turn_back(0, SUM_BANKS[1], late)
             if c >= 2:
-                weigh(0, c - 2)
-            if c == PACK + 3:
-                quantize_z(1, 0)
-            nc.vector.tensor_copy(sup[c][:], h[c][:].indirect(pos2_sb[:]))
-            if c + 1 < R_TILES:
+                loop_weigh(c - 2, HALVES * (c % 2))
+            if c < LAST:
+                pick_sup(c, every)
                 products(c + 1, 1)
-            if casting:
+            if c + LEAD < R_TILES:
                 prepare_w1(c + LEAD)
-            else:
-                round_z(0, c - 2)
             if c == PACK + 2:
-                quantize_z(0, 0)
-        second_stage(0, 0)
-        second_stage(1, 0)
-        gate_tanh(7, every)
-        gate_affine(7, every)
-        weigh(0, 6)
-        round_z(0, 6)
-        weigh(1, 0)
-        weigh(0, 7)
-        round_z(0, 7)
-        for c in range(1, PACK):
-            weigh(1, c)
-        turn_back(0, 1)
-        round_z(1, 3)
-        for c in range(PACK, R_TILES):
-            weigh(1, c)
-        turn_back(1, 1)
-        quantize_z(0, 1)
-        round_z(1, 7)
-        turn_back(2, 0)
-        turn_back(2, 1)
-        second_stage(0, 1)
-        quantize_z(1, 1)
-        second_stage(1, 1)
-        quantize_z(2, 0)
-        quantize_z(2, 1)
-        store(0, (0, 1, 2))
-        second_stage(2, 0)
-        second_stage(2, 1)
-        store(1, (0, 1))
-        store(2, (0, 1))
+                quantize_z(0, early)
+                quantize_z(0, late)
+        pick_sup(LAST, early)
+        pick_sup(LAST, late)
+        make_gate(LAST, early)
+        loop_round(LAST - 2)
+        make_gate(LAST, late)
+        second_stage(0, EARLY_OUT, early)
+        second_stage(0, LATE[0][3], slice(EARLY, EARLY + P))
+        loop_weigh(LAST - 1, 3)
+        loop_round(LAST - 1)
+        loop_weigh(LAST, 1)
+        loop_round(LAST)
+        turn_back(1, SUM_BANKS[1], early)
+
+        spent = [gate[LAST][:, 0:P], gate[LAST][:, P : 2 * P]]
+        for block, sum_bank, last_bank, out_banks in LATE:
+            cols = slice(block * P, (block + 1) * P)
+            if sum_bank == last_bank:
+                sums = [(sum_bank, tuple(range(PACK, R_TILES)))]
+            else:
+                sums = [(sum_bank, tuple(range(PACK, LAST))), (last_bank, (LAST,))]
+            for bank_no, tiles in sums:
+                open_sum(bank_no, tiles, cols)
+            for bank_no, tiles in sums:
+                for c in tiles:
+                    weigh(c, spent[-2], bank_no, tiles, cols)
+                    spent.append(gate[c][:, cols])
+                round_z(bank_no, tiles, cols)
+            turn_back(1, sum_bank, cols)
+        quantize_z(1, early)
+        second_stage(1, EARLY_OUT, early)
+        second_stage(0, LATE[1][3], slice(EARLY + P, PAIRS))
+        for block, sum_bank, last_bank, out_banks in LATE:
+            cols = slice(block * P, (block + 1) * P)
+            quantize_z(1, cols)
+            second_stage(1, out_banks, cols)
+        store(EARLY_OUT, early, (nc.vector.tensor_copy, nc.scalar.copy, nc.vector.tensor_copy))
+        for block, sum_bank, last_bank, out_banks in LATE:
+            cols = slice(block * P, (block + 1) * P)
+            store(out_banks, cols, (nc.scalar.copy, nc.vector.tensor_copy))

@@ -24,20 +24,26 @@ P = 128
 PACK = 4
 K_PASS = P * PACK
 PASSES = 2
+QUADRANT = 32
+SCALE_ROWS = 16
+PER_COLUMN = 16
 BANK = 512
 R_TILES = H // P
+LAST = R_TILES - 1
 N_TILES = N // P
 HALVES = S // BANK
-W2_CHUNK = 2
-LEAD = 2
-ON_VECTOR = ((1, 0), (1, 1))
 BLOCKS = PAIRS // P
 EARLY = 2 * P
-LAST = R_TILES - 1
-SUM_BANKS = (6, 7)
-VEC_BANK = 7
-EARLY_OUT = (2, 3, 4)
-LATE = ((2, 1, 1, (5, 0)), (3, 6, 7, (1, 7)))
+W2_CHUNK = 2
+LEAD = 2
+W1_ON_VECTOR = 1
+SILU_SLOTS = 4
+
+FIRST_STAGE_PAIRS = 3
+TURN_BANKS = (6, 7)
+EARLY_RESULT_BANKS = (2, 3, 4)
+BLOCK2_RESULT_BANKS = (5, 0)
+BLOCK2_TURN_BANK = 1
 
 
 def tile_list_handshape_pair_gloss_kernel(
@@ -46,16 +52,19 @@ def tile_list_handshape_pair_gloss_kernel(
     nc = tc.nc
     with ExitStack() as ctx:
         keep = ctx.enter_context(tc.tile_pool(name="keep", bufs=1))
-        ring = ctx.enter_context(tc.tile_pool(name="ring", bufs=2))
+        ring = ctx.enter_context(tc.tile_pool(name="ring", bufs=LEAD + 1))
         psum = ctx.enter_context(tc.psum_pool(name="psum", bufs=1))
         banks = [psum.tile([P, BANK], F32, name=f"bank{b}") for b in range(8)]
 
         def held(shape, dtype, name):
             return keep.tile(shape, dtype, name=name, align_bytes=64)
 
-        offs_sb = keep.tile([P, S // 16], U16, name="offs_sb")
-        pos1_sb = keep.tile([P, PAIRS // 16], U16, name="pos1_sb")
-        pos2_sb = keep.tile([P, PAIRS // 16], U16, name="pos2_sb")
+        def entries(list_tile, cols):
+            return list_tile[:, cols.start // PER_COLUMN : cols.stop // PER_COLUMN]
+
+        offs_sb = keep.tile([P, S // PER_COLUMN], U16, name="offs_sb")
+        pos1_sb = keep.tile([P, PAIRS // PER_COLUMN], U16, name="pos1_sb")
+        pos2_sb = keep.tile([P, PAIRS // PER_COLUMN], U16, name="pos2_sb")
         tab_scale_rows = held([P, T], U8, "tab_scale_rows")
         tab_word_sb = [held([P, T], U16, f"tab_word{a}") for a in range(PASSES)]
         w2_plane = held([P, PASSES, H], U8, "w2_plane")
@@ -65,29 +74,32 @@ def tile_list_handshape_pair_gloss_kernel(
         vec_rows = held([P, P], F32, "vec_rows")
         ident = held([P, P], F32, "ident")
         gain_col = held([P, R_TILES], F32, "gain_col")
-        steep_col = held([P, R_TILES], F32, "steep_col")
+        half_steep_col = held([P, R_TILES], F32, "half_steep_col")
 
         zeros = held([P, P], F32, "zeros")
         nc.vector.memset(zeros[:], 0.0)
         nc.scalar.activation(vec_rows[:], zeros[:], SILU)
+
+        scale_base = P - PASSES * SCALE_ROWS
         nc.vector.memset(w2_plane[:].rearrange("p a c -> p (a c)").bitcast(I32), 0)
-        nc.vector.memset(tab_scale_rows[0:96, :].bitcast(I32), 0)
+        nc.vector.memset(tab_scale_rows[0:scale_base, :].bitcast(I32), 0)
         for a in range(PASSES):
             nc.vector.memset(picked_plane[a][:].bitcast(I32), 0)
         nc.vector.memset(w3_plane[:].rearrange("p a c -> p (a c)").bitcast(I32), 0)
 
         nc.sync.dma_start(offs_sb[:], offs)
         nc.sync.dma_start(
-            out=tab_scale_rows[96:P, :].bitcast(I32), in_=tab_scales.rearrange("a q t -> (a q) t").bitcast(I32)
+            out=tab_scale_rows[scale_base:P, :].bitcast(I32),
+            in_=tab_scales.rearrange("a q t -> (a q) t").bitcast(I32),
         )
         for a in range(PASSES):
             nc.sync.dma_start(out=tab_word_sb[a][:].bitcast(I32), in_=tab_words[a].bitcast(I32))
 
         def load_plane(queue, plane, scales):
-            for q in range(4):
+            for q in range(PACK):
                 queue.dma_start(
-                    out=plane[32 * q : 32 * q + 4, :, :].bitcast(I32),
-                    in_=scales[:, 4 * q : 4 * q + 4, :].rearrange("a r c -> r a c").bitcast(I32),
+                    out=plane[QUADRANT * q : QUADRANT * q + PACK, :, :].bitcast(I32),
+                    in_=scales[:, PACK * q : PACK * (q + 1), :].rearrange("a r c -> r a c").bitcast(I32),
                 )
 
         load_plane(nc.scalar, w2_plane, w2_scales)
@@ -95,40 +107,44 @@ def tile_list_handshape_pair_gloss_kernel(
         nc.scalar.dma_start(out=vec_rows[R_TILES : 2 * R_TILES, :], in_=steep.rearrange("(c p) -> c p", p=P))
         make_identity(nc, ident[:])
 
-        w2_sb = {}
+        w2_operands = {}
         w1_raw = {}
         w2_view = w2_words.rearrange("a p c t -> p a (c t)")
 
-        def load_w2(c0):
-            tile = held([P, PASSES, W2_CHUNK * P], U32, f"w2_sb{c0}")
-            cols = slice(PACK * P * c0, PACK * P * (c0 + W2_CHUNK))
-            nc.sync.dma_start(out=tile[:].bitcast(I32), in_=w2_view[:, :, cols].bitcast(I32))
+        def load_w2(first):
+            tile = held([P, PASSES, W2_CHUNK * P], U32, f"w2_sb{first}")
+            byte_cols = slice(PACK * P * first, PACK * P * (first + W2_CHUNK))
+            nc.sync.dma_start(out=tile[:].bitcast(I32), in_=w2_view[:, :, byte_cols].bitcast(I32))
             for i in range(W2_CHUNK):
-                w2_sb[c0 + i] = (tile, i * P)
+                c = first + i
+                w2_operands[c] = [
+                    (tile[:, a, i * P : (i + 1) * P], w2_plane[:, a, c * P : (c + 1) * P]) for a in range(PASSES)
+                ]
 
         def load_w1(c):
             for a in range(PASSES):
                 tile = held([P, PACK, P], F32, f"w1_raw{c}_{a}")
                 rows = w1[a * K_PASS : (a + 1) * K_PASS, c * P : (c + 1) * P]
                 nc.sync.dma_start(out=tile[:], in_=rows.rearrange("(p j) c -> p j c", j=PACK))
-                w1_raw[(c, a)] = (tile, 0)
+                w1_raw[(c, a)] = tile
 
         load_w2(0)
         load_w1(0)
 
         nc.vector.tensor_copy(picked_rows[:], tab_scale_rows[:].indirect(offs_sb[:]))
-        for a, queue in ((0, nc.scalar), (1, nc.scalar)):
-            for q in range(4):
-                queue.dma_start(
-                    out=picked_plane[a][32 * q : 32 * q + 4, :].bitcast(I32),
-                    in_=picked_rows[96 + 16 * a + 4 * q : 96 + 16 * a + 4 * q + 4, :].bitcast(I32),
+        for a in range(PASSES):
+            for q in range(PACK):
+                row = scale_base + SCALE_ROWS * a + PACK * q
+                nc.scalar.dma_start(
+                    out=picked_plane[a][QUADRANT * q : QUADRANT * q + PACK, :].bitcast(I32),
+                    in_=picked_rows[row : row + PACK, :].bitcast(I32),
                 )
         picked = {}
         for a in range(PASSES):
             for half in range(HALVES):
                 tile = held([P, BANK], U16, f"picked{a}_{half}")
-                part = offs_sb[:, half * BANK // 16 : (half + 1) * BANK // 16]
-                nc.vector.tensor_copy(tile[:], tab_word_sb[a][:].indirect(part))
+                offsets = entries(offs_sb, slice(half * BANK, (half + 1) * BANK))
+                nc.vector.tensor_copy(tile[:], tab_word_sb[a][:].indirect(offsets))
                 picked[(a, half)] = tile
 
         load_w1(1)
@@ -144,86 +160,92 @@ def tile_list_handshape_pair_gloss_kernel(
         nc.sync.dma_start(out=w3_sb[:].bitcast(I32), in_=w3_words.rearrange("a p b -> p a b").bitcast(I32))
         load_plane(nc.sync, w3_plane, w3_scales)
 
-        w1_bf = {}
-        w1_q = {}
+        w1_operands = {}
 
-        def round_w1(c):
-            grouped = ring.tile([P, PASSES, P, PACK], BF16, name="w1_grouped", align_bytes=64, bufs=LEAD + 1)
+        def prepare_w1(c):
+            grouped = ring.tile([P, PASSES, P, PACK], BF16, name="w1_grouped", align_bytes=64)
+            copy = nc.vector.tensor_copy if c == W1_ON_VECTOR else nc.scalar.copy
             for a in range(PASSES):
-                tile, col = w1_raw[(c, a)]
-                copy = nc.vector.tensor_copy if (c, a) in ON_VECTOR else nc.scalar.copy
                 copy(
-                    grouped[:, a, :, :].rearrange("p (c i) j -> p c j i", i=4),
-                    tile[:, :, col : col + P].rearrange("p j (c i) -> p c j i", i=4),
+                    grouped[:, a, :, :].rearrange("p (c i) j -> p c j i", i=PACK),
+                    w1_raw[(c, a)][:].rearrange("p j (c i) -> p c j i", i=PACK),
                 )
-            w1_bf[c] = grouped
-
-        def quantize_w1(c):
             codes = held([P, PASSES * P], U32, f"w1_codes{c}")
             plane = held([P, PASSES * P], U8, f"w1_plane{c}")
             nc.vector.quantize_mx(
-                out=codes[:].bitcast(FP8X4), scales=plane[:], in_=w1_bf[c][:].rearrange("p a c j -> p (a c j)")
+                out=codes[:].bitcast(FP8X4), scales=plane[:], in_=grouped[:].rearrange("p a c j -> p (a c j)")
             )
-            w1_q[c] = (codes, plane)
+            w1_operands[c] = [(codes[:, a * P : (a + 1) * P], plane[:, a * P : (a + 1) * P]) for a in range(PASSES)]
 
-        def first_stage(bank, weights, half, order):
-            cols = slice(half * BANK, (half + 1) * BANK)
-            for a in order:
-                codes, plane = weights[a]
+        def table_product(bank_no, operands, half, passes):
+            for a in passes:
+                codes, plane = operands[a]
                 nc.tensor.matmul_mx(
-                    out=bank[:],
+                    out=banks[bank_no][:],
                     lhsT=codes.bitcast(FP8X4),
                     lhsT_scale=plane,
                     rhs=picked[(a, half)][:].bitcast(FP4X4),
-                    rhs_scale=picked_plane[a][:, cols],
-                    start=(a == order[0]),
-                    stop=(a == order[-1]),
+                    rhs_scale=picked_plane[a][:, half * BANK : (half + 1) * BANK],
+                    start=(a == passes[0]),
+                    stop=(a == passes[-1]),
                 )
 
         h = [held([P, S], F32, f"h{c}") for c in range(R_TILES)]
         sup = [held([P, PAIRS], F32, f"sup{c}") for c in range(R_TILES)]
         bend = [held([P, PAIRS], F32, f"bend{c}") for c in range(R_TILES)]
         gate = [held([P, PAIRS], F32, f"gate{c}") for c in range(R_TILES)]
-        acts = held([P, 4, BANK], F32, "acts")
+        silu_buf = held([P, SILU_SLOTS, BANK], F32, "silu_buf")
 
-        def prepare_w1(c):
-            round_w1(c)
-            quantize_w1(c)
+        def bent_bank(c, half):
+            return 2 * ((HALVES * c + half) % FIRST_STAGE_PAIRS)
 
-        def products(c, half, parts=(0, 1)):
-            w2_tile, col = w2_sb[c]
-            w2_ops = [(w2_tile[:, a, col : col + P], w2_plane[:, a, c * P : (c + 1) * P]) for a in range(PASSES)]
-            codes, plane = w1_q[c]
-            w1_ops = [(codes[:, a * P : (a + 1) * P], plane[:, a * P : (a + 1) * P]) for a in range(PASSES)]
-            pair = (HALVES * c + half) % 3
-            for part in parts:
-                first_stage(banks[2 * pair + part], (w2_ops, w1_ops)[part], half, ((0, 1), (1, 0))[part])
+        def silu_slot(c, half):
+            return (HALVES * c + half) % SILU_SLOTS
+
+        def bent_product(c, half):
+            table_product(bent_bank(c, half), w2_operands[c], half, (0, 1))
+
+        def lin_product(c, half):
+            table_product(bent_bank(c, half) + 1, w1_operands[c], half, (1, 0))
 
         def features(c, half):
-            pair = (HALVES * c + half) % 3
-            act = acts[:, (HALVES * c + half) % 4, :]
-            nc.scalar.activation(act, banks[2 * pair][:], SILU)
+            act = silu_buf[:, silu_slot(c, half), :]
+            nc.scalar.activation(act, banks[bent_bank(c, half)][:], SILU)
             nc.vector.scalar_tensor_tensor(
-                h[c][:, half * BANK : (half + 1) * BANK], act, gain_col[:, c : c + 1], banks[2 * pair + 1][:],
-                MULT, ADD,
+                h[c][:, half * BANK : (half + 1) * BANK],
+                act,
+                gain_col[:, c : c + 1],
+                banks[bent_bank(c, half) + 1][:],
+                MULT,
+                ADD,
             )
 
+        def pick_sup(c, cols):
+            nc.vector.tensor_copy(sup[c][:, cols], h[c][:].indirect(entries(pos2_sb, cols)))
+
         def make_gate(c, cols):
-            nc.scalar.activation(bend[c][:, cols], sup[c][:, cols], TANH, scale=steep_col[:, c : c + 1])
+            nc.scalar.activation(bend[c][:, cols], sup[c][:, cols], TANH, scale=half_steep_col[:, c : c + 1])
             nc.scalar.activation(gate[c][:, cols], bend[c][:, cols], COPY, bias=0.5, scale=0.5)
 
-        def pick_sup(c, cols):
-            part = pos2_sb[:, cols.start // 16 : cols.stop // 16]
-            nc.vector.tensor_copy(sup[c][:, cols], h[c][:].indirect(part))
+        every, early, late = slice(0, PAIRS), slice(0, EARLY), slice(EARLY, PAIRS)
+        block2, block3 = slice(EARLY, EARLY + P), slice(EARLY + P, PAIRS)
 
-        out_view = out.rearrange("(t p) m -> p t m", p=P)
-        z_t = [held([P, BLOCKS, 2, P, 2], BF16, f"z_t{a}") for a in range(PASSES)]
-        z_q = {}
+        def blocks_in(cols):
+            return (cols.stop - cols.start) // P
+
+        z_turned = {}
+        for a, cols in ((0, every), (1, early), (1, block2), (1, block3)):
+            tile = held([P, blocks_in(cols), 2, P, 2], BF16, f"z_turned{a}_{cols.start}")
+            for m in range(cols.start, cols.stop, P):
+                z_turned[(a, m)] = (tile, cols.start)
+
+        def z_blocks(a, cols):
+            tile, first = z_turned[(a, cols.start)]
+            return tile[:, (cols.start - first) // P : (cols.stop - first) // P]
 
         def sum_view(bank_no, tiles, cols):
-            blocks = (cols.stop - cols.start) // P
-            used = banks[bank_no][:, 0 : blocks * len(tiles) * P]
-            return used.rearrange("p (b i r) -> p b i r", b=blocks, i=len(tiles))
+            used = banks[bank_no][:, 0 : blocks_in(cols) * len(tiles) * P]
+            return used.rearrange("p (b i r) -> p b i r", b=blocks_in(cols), i=len(tiles))
 
         def open_sum(bank_no, tiles, cols):
             view = sum_view(bank_no, tiles, cols)
@@ -236,157 +258,167 @@ def tile_list_handshape_pair_gloss_kernel(
 
         def weigh(c, gated, bank_no, tiles, cols):
             view = sum_view(bank_no, tiles, cols)
-            blocks = (cols.stop - cols.start) // P
-            part = pos1_sb[:, cols.start // 16 : cols.stop // 16]
-            nc.vector.tensor_tensor(gated, h[c][:].indirect(part), gate[c][:, cols], MULT)
-            for b in range(blocks):
+            nc.vector.tensor_tensor(gated, h[c][:].indirect(entries(pos1_sb, cols)), gate[c][:, cols], MULT)
+            for b in range(blocks_in(cols)):
                 nc.tensor.matmul(
                     view[:, b, tiles.index(c), :], gated[:, b * P : (b + 1) * P], ident[:], start=False,
-                    stop=(c == tiles[-1] and b == blocks - 1), is_transpose=True,
+                    stop=(c == tiles[-1] and b == blocks_in(cols) - 1), is_transpose=True,
                 )
 
         def round_z(bank_no, tiles, cols):
-            q0 = 32 * (tiles[0] % PACK)
+            per_tile = P // PACK
+            q0 = per_tile * (tiles[0] % PACK)
             nc.scalar.copy(
-                z_t[tiles[0] // PACK][:, cols.start // P : cols.stop // P, :, q0 : q0 + 32 * len(tiles), :],
+                z_blocks(tiles[0] // PACK, cols)[:, :, :, q0 : q0 + per_tile * len(tiles), :],
                 sum_view(bank_no, tiles, cols).rearrange("p b i (q u e) -> p b u (i q) e", u=2, e=2),
             )
 
-        z_bf = {}
+        z_grouped = {}
+        z_operands = {}
 
         def turn_back(a, bank_no, cols):
             width = cols.stop - cols.start
-            words = z_t[a][:].rearrange("p b u q e -> p b u (q e)").bitcast(F32)
+            words = z_blocks(a, cols).rearrange("p b u q e -> p b u (q e)").bitcast(F32)
             turned = banks[bank_no][:, 0 : 2 * width].rearrange("p (u m) -> p u m", u=2)
-            for b in range(width // P):
+            for b in range(blocks_in(cols)):
                 for u in range(2):
-                    nc.tensor.transpose(
-                        turned[:, u, b * P : (b + 1) * P], words[:, cols.start // P + b, u, :], ident[:]
-                    )
-            tile = held([P, PACK * width], BF16, f"z_bf{a}_{cols.start}")
+                    nc.tensor.transpose(turned[:, u, b * P : (b + 1) * P], words[:, b, u, :], ident[:])
+            tile = held([P, PACK * width], BF16, f"z_grouped{a}_{cols.start}")
             nc.scalar.copy(
                 tile[:].bitcast(F32).rearrange("p (m u) -> p m u", u=2), turned.rearrange("p u m -> p m u")
             )
-            z_bf[(a, cols.start)] = tile
+            z_grouped[(a, cols.start)] = tile
 
         def quantize_z(a, cols):
             width = cols.stop - cols.start
-            z_codes = held([P, width], U32, f"z_codes{a}_{cols.start}")
-            z_plane = held([P, width], U8, f"z_plane{a}_{cols.start}")
-            nc.vector.quantize_mx(out=z_codes[:].bitcast(FP8X4), scales=z_plane[:], in_=z_bf[(a, cols.start)][:])
-            for b in range(width // P):
-                z_q[(a, cols.start // P + b)] = (z_codes[:, b * P : (b + 1) * P], z_plane[:, b * P : (b + 1) * P])
+            codes = held([P, width], U32, f"z_codes{a}_{cols.start}")
+            plane = held([P, width], U8, f"z_plane{a}_{cols.start}")
+            nc.vector.quantize_mx(out=codes[:].bitcast(FP8X4), scales=plane[:], in_=z_grouped[(a, cols.start)][:])
+            for m in range(0, width, P):
+                z_operands[(a, cols.start + m)] = (codes[:, m : m + P], plane[:, m : m + P])
 
-        def result_view(bank_no, out_banks, cols):
+        def result_view(bank_no, result_banks, cols):
             width = cols.stop - cols.start
-            per_bank = N_TILES // len(out_banks)
+            per_bank = N_TILES // len(result_banks)
             return banks[bank_no][:, 0 : per_bank * width].rearrange("p (t m) -> p t m", m=width)
 
-        def second_stage(a, out_banks, cols):
-            blocks = (cols.stop - cols.start) // P
-            per_bank = N_TILES // len(out_banks)
-            for slot, bank_no in enumerate(out_banks):
-                acc = result_view(bank_no, out_banks, cols)
+        def second_stage(a, result_banks, cols):
+            per_bank = N_TILES // len(result_banks)
+            for slot, bank_no in enumerate(result_banks):
+                acc = result_view(bank_no, result_banks, cols)
                 for i in range(per_bank):
                     n = slot * per_bank + i
-                    for b in range(blocks):
-                        z_codes, z_plane = z_q[(a, cols.start // P + b)]
+                    for b in range(blocks_in(cols)):
+                        codes, plane = z_operands[(a, cols.start + b * P)]
                         nc.tensor.matmul_mx(
                             out=acc[:, i, b * P : (b + 1) * P],
                             lhsT=w3_sb[:, a, 2 * P * n : 2 * P * (n + 1)].bitcast(FP4X4),
                             lhsT_scale=w3_plane[:, a, P * n : P * (n + 1)],
-                            rhs=z_codes.bitcast(FP8X4),
-                            rhs_scale=z_plane,
+                            rhs=codes.bitcast(FP8X4),
+                            rhs_scale=plane,
                             start=(a == 0 and i == 0 and b == 0),
-                            stop=(a == PASSES - 1 and i == per_bank - 1 and b == blocks - 1),
+                            stop=(a == PASSES - 1 and i == per_bank - 1 and b == blocks_in(cols) - 1),
                         )
 
-        def store(out_banks, cols, copies):
-            per_bank = N_TILES // len(out_banks)
-            for slot, bank_no in enumerate(out_banks):
-                result = held([P, per_bank, cols.stop - cols.start], F32, f"result{cols.start}_{slot}")
-                copies[slot](result[:], result_view(bank_no, out_banks, cols))
-                nc.sync.dma_start(out=out_view[:, slot * per_bank : (slot + 1) * per_bank, cols], in_=result[:])
+        out_view = out.rearrange("(t p) m -> p t m", p=P)
 
-        every, early, late = slice(0, PAIRS), slice(0, EARLY), slice(EARLY, PAIRS)
+        def store(result_banks, cols, copies):
+            per_bank = N_TILES // len(result_banks)
+            for slot, bank_no in enumerate(result_banks):
+                result = held([P, per_bank, cols.stop - cols.start], F32, f"result{cols.start}_{slot}")
+                copies[slot](result[:], result_view(bank_no, result_banks, cols))
+                nc.sync.dma_start(out=out_view[:, slot * per_bank : (slot + 1) * per_bank, cols], in_=result[:])
 
         def loop_cols(c):
             return every if c < PACK else early
 
         def loop_weigh(c, slot):
             cols = loop_cols(c)
-            open_sum(SUM_BANKS[c % 2], (c,), cols)
-            weigh(c, acts[:, slot, 0 : cols.stop], SUM_BANKS[c % 2], (c,), cols)
+            open_sum(TURN_BANKS[c % 2], (c,), cols)
+            weigh(c, silu_buf[:, slot, cols], TURN_BANKS[c % 2], (c,), cols)
 
         def loop_round(c):
-            round_z(SUM_BANKS[c % 2], (c,), loop_cols(c))
+            round_z(TURN_BANKS[c % 2], (c,), loop_cols(c))
 
-        prepare_w1(0)
-        prepare_w1(1)
-        nc.tensor.transpose(banks[VEC_BANK][:, 0:P], vec_rows[:], ident[:])
-        nc.scalar.copy(gain_col[:], banks[VEC_BANK][:, 0:R_TILES])
-        nc.scalar.activation(steep_col[:], banks[VEC_BANK][:, R_TILES : 2 * R_TILES], COPY, scale=0.5)
-        for part in range(2):
+        for c in range(LEAD):
+            prepare_w1(c)
+        vec_cols = banks[TURN_BANKS[1]]
+        nc.tensor.transpose(vec_cols[:, 0:P], vec_rows[:], ident[:])
+        nc.scalar.copy(gain_col[:], vec_cols[:, 0:R_TILES])
+        nc.scalar.activation(half_steep_col[:], vec_cols[:, R_TILES : 2 * R_TILES], COPY, scale=0.5)
+        for product in (bent_product, lin_product):
             for half in range(HALVES):
-                products(0, half, (part,))
+                product(0, half)
+
+        pass0_round = PACK - 1 + 3
         for c in range(R_TILES):
             features(c, 0)
             if c < LAST:
-                products(c + 1, 0)
+                bent_product(c + 1, 0)
+                lin_product(c + 1, 0)
             features(c, 1)
             if c >= 1:
                 make_gate(c - 1, every)
             if c >= 3:
                 loop_round(c - 3)
-            if c == PACK + 2:
-                turn_back(0, SUM_BANKS[0], early)
-                turn_back(0, SUM_BANKS[1], late)
+            if c == pass0_round:
+                turn_back(0, TURN_BANKS[0], early)
+                turn_back(0, TURN_BANKS[1], late)
             if c >= 2:
-                loop_weigh(c - 2, HALVES * (c % 2))
+                loop_weigh(c - 2, silu_slot(c, 0))
             if c < LAST:
                 pick_sup(c, every)
-                products(c + 1, 1)
+                bent_product(c + 1, 1)
+                lin_product(c + 1, 1)
             if c + LEAD < R_TILES:
                 prepare_w1(c + LEAD)
-            if c == PACK + 2:
+            if c == pass0_round:
                 quantize_z(0, early)
                 quantize_z(0, late)
+
         pick_sup(LAST, early)
         pick_sup(LAST, late)
         make_gate(LAST, early)
         loop_round(LAST - 2)
         make_gate(LAST, late)
-        second_stage(0, EARLY_OUT, early)
-        second_stage(0, LATE[0][3], slice(EARLY, EARLY + P))
-        loop_weigh(LAST - 1, 3)
+        second_stage(0, EARLY_RESULT_BANKS, early)
+        second_stage(0, BLOCK2_RESULT_BANKS, block2)
+        loop_weigh(LAST - 1, silu_slot(LAST, 1))
         loop_round(LAST - 1)
-        loop_weigh(LAST, 1)
+        loop_weigh(LAST, silu_slot(LAST - 1, 1))
         loop_round(LAST)
-        turn_back(1, SUM_BANKS[1], early)
-
-        spent = [gate[LAST][:, 0:P], gate[LAST][:, P : 2 * P]]
-        for block, sum_bank, last_bank, out_banks in LATE:
-            cols = slice(block * P, (block + 1) * P)
-            if sum_bank == last_bank:
-                sums = [(sum_bank, tuple(range(PACK, R_TILES)))]
-            else:
-                sums = [(sum_bank, tuple(range(PACK, LAST))), (last_bank, (LAST,))]
-            for bank_no, tiles in sums:
-                open_sum(bank_no, tiles, cols)
-            for bank_no, tiles in sums:
-                for c in tiles:
-                    weigh(c, spent[-2], bank_no, tiles, cols)
-                    spent.append(gate[c][:, cols])
-                round_z(bank_no, tiles, cols)
-            turn_back(1, sum_bank, cols)
+        turn_back(1, TURN_BANKS[0], early)
         quantize_z(1, early)
-        second_stage(1, EARLY_OUT, early)
-        second_stage(0, LATE[1][3], slice(EARLY + P, PAIRS))
-        for block, sum_bank, last_bank, out_banks in LATE:
-            cols = slice(block * P, (block + 1) * P)
+
+        upper = tuple(range(PACK, R_TILES))
+        front, back = upper[:2], upper[2:]
+        early_turned = z_blocks(1, early).rearrange("p b u q e -> p (b u q e)").bitcast(F32)
+        early_grouped = z_grouped[(1, early.start)][:].bitcast(F32)
+        block3_bank, last_bank = TURN_BANKS[1], TURN_BANKS[0]
+        open_sum(BLOCK2_TURN_BANK, upper, block2)
+        open_sum(block3_bank, upper[:-1], block3)
+        for i, c in enumerate(front):
+            weigh(c, gate[LAST][:, i * P : (i + 1) * P], BLOCK2_TURN_BANK, upper, block2)
+        for c in front:
+            weigh(c, gate[c][:, block2], block3_bank, upper[:-1], block3)
+        for i, c in enumerate(back):
+            weigh(c, early_turned[:, i * P : (i + 1) * P], BLOCK2_TURN_BANK, upper, block2)
+        round_z(BLOCK2_TURN_BANK, upper, block2)
+        turn_back(1, BLOCK2_TURN_BANK, block2)
+        open_sum(last_bank, upper[-1:], block3)
+        for i, (bank_no, tiles) in enumerate(((block3_bank, upper[:-1]), (last_bank, upper[-1:]))):
+            weigh(tiles[-1], early_grouped[:, i * P : (i + 1) * P], bank_no, tiles, block3)
+            round_z(bank_no, tiles, block3)
+        turn_back(1, block3_bank, block3)
+
+        block3_result_banks = (BLOCK2_TURN_BANK, last_bank)
+        late_groups = ((BLOCK2_RESULT_BANKS, block2), (block3_result_banks, block3))
+        second_stage(1, EARLY_RESULT_BANKS, early)
+        second_stage(0, block3_result_banks, block3)
+        for result_banks, cols in late_groups:
             quantize_z(1, cols)
-            second_stage(1, out_banks, cols)
-        store(EARLY_OUT, early, (nc.vector.tensor_copy, nc.scalar.copy, nc.vector.tensor_copy))
-        for block, sum_bank, last_bank, out_banks in LATE:
-            cols = slice(block * P, (block + 1) * P)
-            store(out_banks, cols, (nc.scalar.copy, nc.vector.tensor_copy))
+            second_stage(1, result_banks, cols)
+
+        store(EARLY_RESULT_BANKS, early, [nc.vector.tensor_copy] * len(EARLY_RESULT_BANKS))
+        for result_banks, cols in late_groups:
+            store(result_banks, cols, (nc.scalar.copy, nc.vector.tensor_copy))

from contextlib import ExitStack

import concourse.mybir as mybir
from concourse.masks import make_identity

K, T, S, PAIRS, H, N = 1024, 4096, 1024, 512, 1024, 768
FLOPS = 2 * 2 * K * H * S + 2 * H * N * PAIRS

F32 = mybir.dt.float32
BF16 = mybir.dt.bfloat16
I32 = mybir.dt.int32
U32 = mybir.dt.uint32
U16 = mybir.dt.uint16
U8 = mybir.dt.uint8
FP8X4 = mybir.dt.float8_e4m3fn_x4
FP4X4 = mybir.dt.float4_e2m1fn_x4
MULT = mybir.AluOpType.mult
ADD = mybir.AluOpType.add
SILU = mybir.ActivationFunctionType.Silu
TANH = mybir.ActivationFunctionType.Tanh
COPY = mybir.ActivationFunctionType.Copy

P = 128
PACK = 4
K_PASS = P * PACK
PASSES = 2
QUADRANT = 32
SCALE_ROWS = 16
PER_COLUMN = 16
BANK = 512
R_TILES = H // P
LAST = R_TILES - 1
N_TILES = N // P
HALVES = S // BANK
BLOCKS = PAIRS // P
EARLY = 2 * P
W2_CHUNK = 2
LEAD = 2
W1_ON_VECTOR = 1
SILU_SLOTS = 4

FIRST_STAGE_PAIRS = 3
TURN_BANKS = (6, 7)
EARLY_RESULT_BANKS = (2, 3, 4)
BLOCK2_RESULT_BANKS = (5, 0)
BLOCK2_TURN_BANK = 1


def tile_list_handshape_pair_gloss_kernel(
    tc, tab_words, tab_scales, offs, pos1, pos2, w1, w2_words, w2_scales, gain, steep, w3_words, w3_scales, out
):
    nc = tc.nc
    with ExitStack() as ctx:
        keep = ctx.enter_context(tc.tile_pool(name="keep", bufs=1))
        ring = ctx.enter_context(tc.tile_pool(name="ring", bufs=LEAD + 1))
        psum = ctx.enter_context(tc.psum_pool(name="psum", bufs=1))
        banks = [psum.tile([P, BANK], F32, name=f"bank{b}") for b in range(8)]

        def held(shape, dtype, name):
            return keep.tile(shape, dtype, name=name, align_bytes=64)

        def entries(list_tile, cols):
            return list_tile[:, cols.start // PER_COLUMN : cols.stop // PER_COLUMN]

        offs_sb = keep.tile([P, S // PER_COLUMN], U16, name="offs_sb")
        pos1_sb = keep.tile([P, PAIRS // PER_COLUMN], U16, name="pos1_sb")
        pos2_sb = keep.tile([P, PAIRS // PER_COLUMN], U16, name="pos2_sb")
        tab_scale_rows = held([P, T], U8, "tab_scale_rows")
        tab_word_sb = [held([P, T], U16, f"tab_word{a}") for a in range(PASSES)]
        w2_plane = held([P, PASSES, H], U8, "w2_plane")
        w3_plane = held([P, PASSES, N], U8, "w3_plane")
        picked_rows = held([P, S], U8, "picked_rows")
        picked_plane = [held([P, S], U8, f"picked_plane{a}") for a in range(PASSES)]
        vec_rows = held([P, P], F32, "vec_rows")
        ident = held([P, P], F32, "ident")
        gain_col = held([P, R_TILES], F32, "gain_col")
        half_steep_col = held([P, R_TILES], F32, "half_steep_col")

        zeros = held([P, P], F32, "zeros")
        nc.vector.memset(zeros[:], 0.0)
        nc.scalar.activation(vec_rows[:], zeros[:], SILU)

        scale_base = P - PASSES * SCALE_ROWS
        nc.vector.memset(w2_plane[:].rearrange("p a c -> p (a c)").bitcast(I32), 0)
        nc.vector.memset(tab_scale_rows[0:scale_base, :].bitcast(I32), 0)
        for a in range(PASSES):
            nc.vector.memset(picked_plane[a][:].bitcast(I32), 0)
        nc.vector.memset(w3_plane[:].rearrange("p a c -> p (a c)").bitcast(I32), 0)

        nc.sync.dma_start(offs_sb[:], offs)
        nc.sync.dma_start(
            out=tab_scale_rows[scale_base:P, :].bitcast(I32),
            in_=tab_scales.rearrange("a q t -> (a q) t").bitcast(I32),
        )
        for a in range(PASSES):
            nc.sync.dma_start(out=tab_word_sb[a][:].bitcast(I32), in_=tab_words[a].bitcast(I32))

        def load_plane(queue, plane, scales):
            for q in range(PACK):
                queue.dma_start(
                    out=plane[QUADRANT * q : QUADRANT * q + PACK, :, :].bitcast(I32),
                    in_=scales[:, PACK * q : PACK * (q + 1), :].rearrange("a r c -> r a c").bitcast(I32),
                )

        load_plane(nc.scalar, w2_plane, w2_scales)
        nc.scalar.dma_start(out=vec_rows[0:R_TILES, :], in_=gain.rearrange("(c p) -> c p", p=P))
        nc.scalar.dma_start(out=vec_rows[R_TILES : 2 * R_TILES, :], in_=steep.rearrange("(c p) -> c p", p=P))
        make_identity(nc, ident[:])

        w2_operands = {}
        w1_raw = {}
        w2_view = w2_words.rearrange("a p c t -> p a (c t)")

        def load_w2(first):
            tile = held([P, PASSES, W2_CHUNK * P], U32, f"w2_sb{first}")
            byte_cols = slice(PACK * P * first, PACK * P * (first + W2_CHUNK))
            nc.sync.dma_start(out=tile[:].bitcast(I32), in_=w2_view[:, :, byte_cols].bitcast(I32))
            for i in range(W2_CHUNK):
                c = first + i
                w2_operands[c] = [
                    (tile[:, a, i * P : (i + 1) * P], w2_plane[:, a, c * P : (c + 1) * P]) for a in range(PASSES)
                ]

        def load_w1(c):
            for a in range(PASSES):
                tile = held([P, PACK, P], F32, f"w1_raw{c}_{a}")
                rows = w1[a * K_PASS : (a + 1) * K_PASS, c * P : (c + 1) * P]
                nc.sync.dma_start(out=tile[:], in_=rows.rearrange("(p j) c -> p j c", j=PACK))
                w1_raw[(c, a)] = tile

        load_w2(0)
        load_w1(0)

        nc.vector.tensor_copy(picked_rows[:], tab_scale_rows[:].indirect(offs_sb[:]))
        for a in range(PASSES):
            for q in range(PACK):
                row = scale_base + SCALE_ROWS * a + PACK * q
                nc.scalar.dma_start(
                    out=picked_plane[a][QUADRANT * q : QUADRANT * q + PACK, :].bitcast(I32),
                    in_=picked_rows[row : row + PACK, :].bitcast(I32),
                )
        picked = {}
        for a in range(PASSES):
            for half in range(HALVES):
                tile = held([P, BANK], U16, f"picked{a}_{half}")
                offsets = entries(offs_sb, slice(half * BANK, (half + 1) * BANK))
                nc.vector.tensor_copy(tile[:], tab_word_sb[a][:].indirect(offsets))
                picked[(a, half)] = tile

        load_w1(1)
        nc.sync.dma_start(pos2_sb[:], pos2)
        load_w1(2)
        load_w2(2)
        nc.sync.dma_start(pos1_sb[:], pos1)
        for c in range(3, R_TILES):
            load_w1(c)
            if c % W2_CHUNK == 0:
                load_w2(c)
        w3_sb = held([P, PASSES, 2 * N], U8, "w3_sb")
        nc.sync.dma_start(out=w3_sb[:].bitcast(I32), in_=w3_words.rearrange("a p b -> p a b").bitcast(I32))
        load_plane(nc.sync, w3_plane, w3_scales)

        w1_operands = {}

        def prepare_w1(c):
            grouped = ring.tile([P, PASSES, P, PACK], BF16, name="w1_grouped", align_bytes=64)
            copy = nc.vector.tensor_copy if c == W1_ON_VECTOR else nc.scalar.copy
            for a in range(PASSES):
                copy(
                    grouped[:, a, :, :].rearrange("p (c i) j -> p c j i", i=PACK),
                    w1_raw[(c, a)][:].rearrange("p j (c i) -> p c j i", i=PACK),
                )
            codes = held([P, PASSES * P], U32, f"w1_codes{c}")
            plane = held([P, PASSES * P], U8, f"w1_plane{c}")
            nc.vector.quantize_mx(
                out=codes[:].bitcast(FP8X4), scales=plane[:], in_=grouped[:].rearrange("p a c j -> p (a c j)")
            )
            w1_operands[c] = [(codes[:, a * P : (a + 1) * P], plane[:, a * P : (a + 1) * P]) for a in range(PASSES)]

        def table_product(bank_no, operands, half, passes):
            for a in passes:
                codes, plane = operands[a]
                nc.tensor.matmul_mx(
                    out=banks[bank_no][:],
                    lhsT=codes.bitcast(FP8X4),
                    lhsT_scale=plane,
                    rhs=picked[(a, half)][:].bitcast(FP4X4),
                    rhs_scale=picked_plane[a][:, half * BANK : (half + 1) * BANK],
                    start=(a == passes[0]),
                    stop=(a == passes[-1]),
                )

        h = [held([P, S], F32, f"h{c}") for c in range(R_TILES)]
        sup = [held([P, PAIRS], F32, f"sup{c}") for c in range(R_TILES)]
        bend = [held([P, PAIRS], F32, f"bend{c}") for c in range(R_TILES)]
        gate = [held([P, PAIRS], F32, f"gate{c}") for c in range(R_TILES)]
        silu_buf = held([P, SILU_SLOTS, BANK], F32, "silu_buf")

        def bent_bank(c, half):
            return 2 * ((HALVES * c + half) % FIRST_STAGE_PAIRS)

        def silu_slot(c, half):
            return (HALVES * c + half) % SILU_SLOTS

        def bent_product(c, half):
            table_product(bent_bank(c, half), w2_operands[c], half, (0, 1))

        def lin_product(c, half):
            table_product(bent_bank(c, half) + 1, w1_operands[c], half, (1, 0))

        def features(c, half):
            act = silu_buf[:, silu_slot(c, half), :]
            nc.scalar.activation(act, banks[bent_bank(c, half)][:], SILU)
            nc.vector.scalar_tensor_tensor(
                h[c][:, half * BANK : (half + 1) * BANK],
                act,
                gain_col[:, c : c + 1],
                banks[bent_bank(c, half) + 1][:],
                MULT,
                ADD,
            )

        def pick_sup(c, cols):
            nc.vector.tensor_copy(sup[c][:, cols], h[c][:].indirect(entries(pos2_sb, cols)))

        def make_gate(c, cols):
            nc.scalar.activation(bend[c][:, cols], sup[c][:, cols], TANH, scale=half_steep_col[:, c : c + 1])
            nc.scalar.activation(gate[c][:, cols], bend[c][:, cols], COPY, bias=0.5, scale=0.5)

        every, early, late = slice(0, PAIRS), slice(0, EARLY), slice(EARLY, PAIRS)
        block2, block3 = slice(EARLY, EARLY + P), slice(EARLY + P, PAIRS)

        def blocks_in(cols):
            return (cols.stop - cols.start) // P

        z_turned = {}
        for a, cols in ((0, every), (1, early), (1, block2), (1, block3)):
            tile = held([P, blocks_in(cols), 2, P, 2], BF16, f"z_turned{a}_{cols.start}")
            for m in range(cols.start, cols.stop, P):
                z_turned[(a, m)] = (tile, cols.start)

        def z_blocks(a, cols):
            tile, first = z_turned[(a, cols.start)]
            return tile[:, (cols.start - first) // P : (cols.stop - first) // P]

        def sum_view(bank_no, tiles, cols):
            used = banks[bank_no][:, 0 : blocks_in(cols) * len(tiles) * P]
            return used.rearrange("p (b i r) -> p b i r", b=blocks_in(cols), i=len(tiles))

        def open_sum(bank_no, tiles, cols):
            view = sum_view(bank_no, tiles, cols)
            for i, c in enumerate(tiles):
                for b, m in enumerate(range(cols.start, cols.stop, P)):
                    nc.tensor.matmul(
                        view[:, b, i, :], sup[c][:, m : m + P], ident[:], start=(i == 0 and b == 0), stop=False,
                        is_transpose=True,
                    )

        def weigh(c, gated, bank_no, tiles, cols):
            view = sum_view(bank_no, tiles, cols)
            nc.vector.tensor_tensor(gated, h[c][:].indirect(entries(pos1_sb, cols)), gate[c][:, cols], MULT)
            for b in range(blocks_in(cols)):
                nc.tensor.matmul(
                    view[:, b, tiles.index(c), :], gated[:, b * P : (b + 1) * P], ident[:], start=False,
                    stop=(c == tiles[-1] and b == blocks_in(cols) - 1), is_transpose=True,
                )

        def round_z(bank_no, tiles, cols):
            per_tile = P // PACK
            q0 = per_tile * (tiles[0] % PACK)
            nc.scalar.copy(
                z_blocks(tiles[0] // PACK, cols)[:, :, :, q0 : q0 + per_tile * len(tiles), :],
                sum_view(bank_no, tiles, cols).rearrange("p b i (q u e) -> p b u (i q) e", u=2, e=2),
            )

        z_grouped = {}
        z_operands = {}

        def turn_back(a, bank_no, cols):
            width = cols.stop - cols.start
            words = z_blocks(a, cols).rearrange("p b u q e -> p b u (q e)").bitcast(F32)
            turned = banks[bank_no][:, 0 : 2 * width].rearrange("p (u m) -> p u m", u=2)
            for b in range(blocks_in(cols)):
                for u in range(2):
                    nc.tensor.transpose(turned[:, u, b * P : (b + 1) * P], words[:, b, u, :], ident[:])
            tile = held([P, PACK * width], BF16, f"z_grouped{a}_{cols.start}")
            nc.scalar.copy(
                tile[:].bitcast(F32).rearrange("p (m u) -> p m u", u=2), turned.rearrange("p u m -> p m u")
            )
            z_grouped[(a, cols.start)] = tile

        def quantize_z(a, cols):
            width = cols.stop - cols.start
            codes = held([P, width], U32, f"z_codes{a}_{cols.start}")
            plane = held([P, width], U8, f"z_plane{a}_{cols.start}")
            nc.vector.quantize_mx(out=codes[:].bitcast(FP8X4), scales=plane[:], in_=z_grouped[(a, cols.start)][:])
            for m in range(0, width, P):
                z_operands[(a, cols.start + m)] = (codes[:, m : m + P], plane[:, m : m + P])

        def result_view(bank_no, result_banks, cols):
            width = cols.stop - cols.start
            per_bank = N_TILES // len(result_banks)
            return banks[bank_no][:, 0 : per_bank * width].rearrange("p (t m) -> p t m", m=width)

        def second_stage(a, result_banks, cols):
            per_bank = N_TILES // len(result_banks)
            for slot, bank_no in enumerate(result_banks):
                acc = result_view(bank_no, result_banks, cols)
                for i in range(per_bank):
                    n = slot * per_bank + i
                    for b in range(blocks_in(cols)):
                        codes, plane = z_operands[(a, cols.start + b * P)]
                        nc.tensor.matmul_mx(
                            out=acc[:, i, b * P : (b + 1) * P],
                            lhsT=w3_sb[:, a, 2 * P * n : 2 * P * (n + 1)].bitcast(FP4X4),
                            lhsT_scale=w3_plane[:, a, P * n : P * (n + 1)],
                            rhs=codes.bitcast(FP8X4),
                            rhs_scale=plane,
                            start=(a == 0 and i == 0 and b == 0),
                            stop=(a == PASSES - 1 and i == per_bank - 1 and b == blocks_in(cols) - 1),
                        )

        out_view = out.rearrange("(t p) m -> p t m", p=P)

        def store(result_banks, cols, copies):
            per_bank = N_TILES // len(result_banks)
            for slot, bank_no in enumerate(result_banks):
                result = held([P, per_bank, cols.stop - cols.start], F32, f"result{cols.start}_{slot}")
                copies[slot](result[:], result_view(bank_no, result_banks, cols))
                nc.sync.dma_start(out=out_view[:, slot * per_bank : (slot + 1) * per_bank, cols], in_=result[:])

        def loop_cols(c):
            return every if c < PACK else early

        def loop_weigh(c, slot):
            cols = loop_cols(c)
            open_sum(TURN_BANKS[c % 2], (c,), cols)
            weigh(c, silu_buf[:, slot, cols], TURN_BANKS[c % 2], (c,), cols)

        def loop_round(c):
            round_z(TURN_BANKS[c % 2], (c,), loop_cols(c))

        for c in range(LEAD):
            prepare_w1(c)
        vec_cols = banks[TURN_BANKS[1]]
        nc.tensor.transpose(vec_cols[:, 0:P], vec_rows[:], ident[:])
        nc.scalar.copy(gain_col[:], vec_cols[:, 0:R_TILES])
        nc.scalar.activation(half_steep_col[:], vec_cols[:, R_TILES : 2 * R_TILES], COPY, scale=0.5)
        for product in (bent_product, lin_product):
            for half in range(HALVES):
                product(0, half)

        pass0_round = PACK - 1 + 3
        for c in range(R_TILES):
            features(c, 0)
            if c < LAST:
                bent_product(c + 1, 0)
                lin_product(c + 1, 0)
            features(c, 1)
            if c >= 1:
                make_gate(c - 1, every)
            if c >= 3:
                loop_round(c - 3)
            if c == pass0_round:
                turn_back(0, TURN_BANKS[0], early)
                turn_back(0, TURN_BANKS[1], late)
            if c >= 2:
                loop_weigh(c - 2, silu_slot(c, 0))
            if c < LAST:
                pick_sup(c, every)
                bent_product(c + 1, 1)
                lin_product(c + 1, 1)
            if c + LEAD < R_TILES:
                prepare_w1(c + LEAD)
            if c == pass0_round:
                quantize_z(0, early)
                quantize_z(0, late)

        pick_sup(LAST, early)
        pick_sup(LAST, late)
        make_gate(LAST, early)
        loop_round(LAST - 2)
        make_gate(LAST, late)
        second_stage(0, EARLY_RESULT_BANKS, early)
        second_stage(0, BLOCK2_RESULT_BANKS, block2)
        loop_weigh(LAST - 1, silu_slot(LAST, 1))
        loop_round(LAST - 1)
        loop_weigh(LAST, silu_slot(LAST - 1, 1))
        loop_round(LAST)
        turn_back(1, TURN_BANKS[0], early)
        quantize_z(1, early)

        upper = tuple(range(PACK, R_TILES))
        front, back = upper[:2], upper[2:]
        early_turned = z_blocks(1, early).rearrange("p b u q e -> p (b u q e)").bitcast(F32)
        early_grouped = z_grouped[(1, early.start)][:].bitcast(F32)
        block3_bank, last_bank = TURN_BANKS[1], TURN_BANKS[0]
        open_sum(BLOCK2_TURN_BANK, upper, block2)
        open_sum(block3_bank, upper[:-1], block3)
        for i, c in enumerate(front):
            weigh(c, gate[LAST][:, i * P : (i + 1) * P], BLOCK2_TURN_BANK, upper, block2)
        for c in front:
            weigh(c, gate[c][:, block2], block3_bank, upper[:-1], block3)
        for i, c in enumerate(back):
            weigh(c, early_turned[:, i * P : (i + 1) * P], BLOCK2_TURN_BANK, upper, block2)
        round_z(BLOCK2_TURN_BANK, upper, block2)
        turn_back(1, BLOCK2_TURN_BANK, block2)
        open_sum(last_bank, upper[-1:], block3)
        for i, (bank_no, tiles) in enumerate(((block3_bank, upper[:-1]), (last_bank, upper[-1:]))):
            weigh(tiles[-1], early_grouped[:, i * P : (i + 1) * P], bank_no, tiles, block3)
            round_z(bank_no, tiles, block3)
        turn_back(1, block3_bank, block3)

        block3_result_banks = (BLOCK2_TURN_BANK, last_bank)
        late_groups = ((BLOCK2_RESULT_BANKS, block2), (block3_result_banks, block3))
        second_stage(1, EARLY_RESULT_BANKS, early)
        second_stage(0, block3_result_banks, block3)
        for result_banks, cols in late_groups:
            quantize_z(1, cols)
            second_stage(1, result_banks, cols)

        store(EARLY_RESULT_BANKS, early, [nc.vector.tensor_copy] * len(EARLY_RESULT_BANKS))
        for result_banks, cols in late_groups:
            store(result_banks, cols, (nc.scalar.copy, nc.vector.tensor_copy))
